import numpy as np, ml_dtypes
CORES = [48,51,52,55]
N = 4
BF = ml_dtypes.bfloat16
def gentries(a):
    return np.ascontiguousarray(a.reshape(8, 16, -1).transpose(0, 2, 1)).reshape(8, -1)
def gtable(e):
    e = np.asarray(e); return np.ascontiguousarray(e.reshape(8, -1, 16).transpose(0, 2, 1)).reshape(128, -1).astype(np.int32)
V, D, B, C = 2048, 4, 256, 512
NONE = 1 << 24
def ring(n, s, order, step):
    n[order, s] = np.roll(order, -step); n[order, s + 1] = np.roll(order, step)
def mesh(rng, pairs):
    n = np.zeros((N * V, D), np.int64); h = D // 2 - 1
    if pairs:
        q = rng.permutation(N)
        circles = [np.stack([q[i] * V + rng.permutation(B), q[i + 1] * V + rng.permutation(B)], 1).reshape(-1) for i in range(0, N, 2)]
    else:
        circles = [rng.permutation((np.arange(N)[:, None] * V + np.arange(B)).reshape(-1))]
    for o in circles:
        for i in range(h): ring(n, 2 * i, o, 2 * i + 1)
    for r in range(N):
        a = r * V + rng.permutation(B); m = r * V + B + rng.permutation(B); p = r * V + C + rng.permutation(V - C)
        ring(n, 2 * h, np.stack([a, m], 1).reshape(-1), 1)
        at = np.zeros(V - B, bool); at[rng.permutation(V - B)[:B]] = True
        o = np.zeros(V - B, np.int64); o[at] = rng.permutation(m); o[~at] = p
        for i in range(h): ring(n, 2 * i, o, i + 1)
        ring(n, 2 * h, p, h + 1)
    return rng.permuted(n, axis=1)
def planes(rng, *shape):
    p = rng.integers(np.array([-3, -3, -3, -10]), np.array([4, 4, 4, 11]), shape + (3, 4))
    return np.matmul(p.swapaxes(-1, -2), p)
def parts(rng, pairs=False):
    return planes(rng, N, 8, V), rng.integers(-15, 16, (N, 8, V, 3)), np.stack([mesh(rng, pairs) for g in range(8)])
def pack(q, c, n):
    h = np.concatenate([c, np.ones(c.shape[:-1] + (1,), c.dtype)], -1); p = h[..., :, None] * h[..., None, :]
    e = n.reshape(8, N, V, D).transpose(1, 0, 3, 2).reshape(N, 8, D * V)
    return {"qu": np.ascontiguousarray(q.transpose(0, 1, 3, 4, 2)).reshape(N, 128, V).astype(np.float32),
            "po": np.ascontiguousarray(p.transpose(0, 1, 3, 4, 2)).reshape(N, 128, V).astype(np.float32).astype(BF),
            "nb": np.stack([gtable(e[r]) for r in range(N)])}
def setup_inputs(rng):
    return pack(*parts(rng))
def setup_inputs_ties(rng):
    n = parts(rng)[2]; G = np.arange(8)[None, :, None]
    a = planes(rng, 8, 2) + np.array([1, 2])[:, None, None] * np.eye(4, dtype=np.int64); b = rng.integers(-15, 16, (8, 2, 3))
    return pack(a[G, rng.integers(0, 2, (N, 8, V))], b[G, rng.integers(0, 2, (N, 8, V))], n)
def setup_inputs_stars(rng):
    q, c, n = parts(rng); c[..., 0] = np.minimum(c[..., 0], 14)
    for g in range(8):
        m = n[g]; v = rng.permutation((np.arange(N)[:, None] * V + np.arange(B)).reshape(-1)); k = m[v]
        meet = (m[k][:, :, :, None] == k[:, None, None, :]).any((1, 2, 3)); used = np.zeros(N * V, bool); done = 0
        for w in v[~meet]:
            leaf = m[w]; near = np.concatenate([leaf, m[leaf].reshape(-1)])
            if used[near].any(): continue
            used[near] = True; done += 1
            for u in np.append(leaf, w):
                q[u // V, g, u % V] = 0; q[u // V, g, u % V, 0, 3] = q[u // V, g, u % V, 3, 0] = -499; c[u // V, g, u % V, 0] = 15 if u == w else -15
            if done == 4: break
        assert done == 4
    return pack(q, c, n)
def setup_inputs_pairs(rng):
    return pack(*parts(rng, True))
def setup_inputs_heavy(rng):
    n = np.stack([mesh(rng, False) for g in range(8)]); G = np.arange(8)[None, :, None]
    x = rng.integers(0, 9, (N, 8, V, 4, 4)); k = np.tril(x) + np.tril(x, -1).swapaxes(-1, -2)
    s = np.where(G < 4, -1, np.where(G < 6, 1, 1 - 2 * rng.integers(0, 2, (N, 8, V))))
    d = pack(s[..., None, None] * (500 - k), rng.integers(12, 16, (N, 8, V, 3)), n)
    n_all = lists_of(d["nb"]); q_all = whole_meshes(d["qu"]); p_all = whole_meshes(d["po"]); own = np.arange(N * V); large = 0
    for g in range(4):
        m1 = collapse(costs(q_all[g], p_all[g], n_all[g]), n_all[g]); q1 = q_all[g].copy()
        for i in range(D): q1 += np.where(m1[n_all[g, i]] == own, q_all[g][:, n_all[g, i]], 0)
        n2 = m1[n_all[g]]; c2 = np.where(n2 == own, NONE, costs(q1, p_all[g], n2)); m2 = collapse(c2, n2)
        large += np.count_nonzero((m1 == own) & (m2 != own) & (np.min(c2, axis=0) < -(1 << 22)))
    assert large > 0
    return d
def setup_inputs_spread(rng):
    q, c, n = parts(rng); a = (500 >> rng.integers(0, 9, (N, 8, V)))[..., None, None]
    x = rng.integers(-a, a + 1, (N, 8, V, 4, 4)); x = np.where(rng.random((N, 8, V, 1, 1)) < 0.0625, 500 - 1000 * rng.integers(0, 2, x.shape), x)
    q = np.tril(x) + np.tril(x, -1).swapaxes(-1, -2); k = rng.integers(0, 8, c.shape)
    c = np.where(k == 0, 0, np.where(k == 1, 15, np.where(k == 2, -15, c)))
    return pack(q, c, n)
def lists_of(nb):
    return np.stack([gentries(nb[r]).reshape(8, D, V) for r in range(N)], axis=2).reshape(8, D, N * V).astype(np.int64)
def whole_meshes(x):
    return x.astype(np.float64).reshape(N, 8, 16, V).transpose(1, 2, 0, 3).reshape(8, 16, N * V).astype(np.int64)
def check_inputs(d):
    bad = []; q = d["qu"].astype(np.float64).reshape(N, 8, 4, 4, V); p = d["po"].astype(np.float64).reshape(N, 8, 4, 4, V); h = p[:, :, :, 3]
    if not np.isfinite(q).all() or (q != np.rint(q)).any() or (np.abs(q) > 500).any(): bad.append("quadrics: whole numbers of size at most 500")
    if (q != q.transpose(0, 1, 3, 2, 4)).any(): bad.append("quadrics: symmetric")
    if not np.isfinite(p).all() or (h != np.rint(h)).any() or (np.abs(h) > 15).any() or (h[:, :, 3] != 1).any() or (p != h[:, :, :, None] * h[:, :, None]).any(): bad.append("points: products of whole coordinates of size at most 15 and 1")
    n = lists_of(d["nb"]).transpose(0, 2, 1); own = np.arange(N * V)[None, :, None]
    if (n < 0).any() or (n >= N * V).any(): return bad + ["neighbours: in range"]
    s = np.sort(n, axis=2)
    if (n == own).any() or (s[:, :, 1:] == s[:, :, :-1]).any(): bad.append("neighbours: different, not the vertex itself")
    if (np.sort((own * (N * V) + n).reshape(8, -1), axis=1) != np.sort((n * (N * V) + own).reshape(8, -1), axis=1)).any(): bad.append("neighbours: symmetric")
    if ((own // V != n // V) & ((own % V >= B) | (n % V >= B))).any(): bad.append("edges between ranks: columns under B")
    if ((own % V < B) & (n % V >= C)).any(): bad.append("neighbours of columns under B: columns under C")
    return bad
def costs(q, p, n):
    return np.stack([np.sum((q + q[:, n[s]]) * p[:, n[s]], axis=0) for s in range(D)])
def collapse(cost, n):
    own = np.arange(N * V); s = np.argmin(cost, axis=0)
    best = cost[s, own]; first = (best < best[n]) | ((best == best[n]) & (own < n)) | (n == own)
    return np.where(np.all(first, axis=0) & (best < NONE), n[s, own], own)
def reference(qu, po, nb):
    n_all = lists_of(nb); q_all = whole_meshes(qu); p_all = whole_meshes(po); own = np.arange(N * V)
    q1 = q_all.copy(); goal = np.zeros((8, N * V), np.int64)
    for g in range(8):
        n = n_all[g]; q = q_all[g]; p = p_all[g]
        m1 = collapse(costs(q, p, n), n)
        for s in range(D): q1[g] += np.where(m1[n[s]] == own, q[:, n[s]], 0)
        n2 = m1[n]
        m2 = collapse(np.where(n2 == own, NONE, costs(q1[g], p, n2)), n2)
        goal[g] = m2[m1]
    q1 = np.ascontiguousarray(q1.reshape(8, 16, N, V).transpose(2, 0, 1, 3)).reshape(N, 128, V)
    goal = np.ascontiguousarray(goal.reshape(8, N, V).transpose(1, 0, 2))
    return {"q1": q1.astype(np.float32), "goal": goal.astype(np.float32)}

@@ -1,0 +1,718 @@
+from concourse.bass import DstId, RemoteDMATransfer
+from concourse.mybir import AluOpType as A, ActivationFunctionType as F
+
+N, V, NB, NC = 4, 2048, 256, 512
+C0, CW, GB = [0, 256, 512, 1024], [256, 256, 512, 1024], [0, 1024, 2048, 4096]
+HALO1, HALO2 = V + 3 * NB, 16 + V + 3 * NC
+BIG = 65536.0
+NONE = float(1 << 24)
+
+SCRATCH = {
+    "Qw": ("sbuf", [128, 16 + HALO1], "float32"),
+    "Pb": ("sbuf", [128, V], "bfloat16"),
+    "nbi": ("sbuf", [128, 512], "int32"),
+    "W": ("sbuf", [128, HALO1], "bfloat16"),
+    "W1": ("sbuf", [128, HALO2], "bfloat16"),
+    "Bw": ("sbuf", [128, HALO1], "bfloat16"),
+    "Mw": ("sbuf", [128, HALO1], "bfloat16"),
+    "B2w": ("sbuf", [128, HALO2], "bfloat16"),
+    "M2w": ("sbuf", [128, HALO1], "bfloat16"),
+    "L1": ("sbuf", [128, 512], "uint16"),
+    "LQ": ("sbuf", [128, 512], "uint16"),
+    "L2": ("sbuf", [128, 512], "uint16"),
+    "LG": ("sbuf", [128, 128], "uint16"),
+    "posq": ("sbuf", [128, 512], "float32"),
+    "VT": ("sbuf", [128, 512], "float32"),
+    "EQ": ("sbuf", [128, 512], "float32"),
+    "NF": ("sbuf", [128, 128], "float32"),
+    "mA": ("sbuf", [128, 128], "float32"),
+    "mB": ("sbuf", [128, 384], "float32"),
+    "GA": ("sbuf", [128, 8192], "bfloat16"),
+    "GB": ("sbuf", [128, 8192], "bfloat16"),
+    "GH": ("sbuf", [128, 8192], "float16"),
+    "PR": ("sbuf", [128, 8192], "float32"),
+    "PRS": ("sbuf", [128, V], "float32"),
+    "C1f": ("sbuf", [128, V], "float32"),
+    "DS": ("sbuf", [128, V], "bfloat16"),
+    "DB": ("sbuf", [128, V], "bfloat16"),
+    "DM": ("sbuf", [128, V], "bfloat16"),
+    "TB": ("sbuf", [128, V], "bfloat16"),
+    "ON": ("sbuf", [128, 512], "bfloat16"),
+    "Id": ("sbuf", [128, 128], "bfloat16"),
+    "PM": ("sbuf", [128, 128], "bfloat16"),
+    "PMh": ("sbuf", [128, 128], "float16"),
+    "PMf": ("sbuf", [128, 128], "float32"),
+    "PI": ("sbuf", [128, 128], "bfloat16"),
+    "E8": ("sbuf", [128, 8], "bfloat16"),
+    "wC": ("sbuf", [128, 8], "float32"),
+    "wS": ("sbuf", [128, 8], "float32"),
+    "wK": ("sbuf", [128, 32], "bfloat16"),
+    "wKf": ("sbuf", [128, 32], "float32"),
+    "ci": ("sbuf", [128, 8], "int32"),
+    "cf": ("sbuf", [128, 32], "float32"),
+    "VC": ("sbuf", [128, 128], "float32"),
+    "VK1": ("sbuf", [128, 512], "float32"),
+    "VK2": ("sbuf", [128, 512], "float32"),
+    "t1": ("sbuf", [128, 256], "float32"),
+    "t2": ("sbuf", [128, 256], "float32"),
+    "best": ("sbuf", [128, 128], "float32"),
+    "rem": ("sbuf", [128, 128], "float32"),
+    "E": ("sbuf", [128, 512], "float32"),
+    "X": ("sbuf", [128, 512], "float32"),
+    "X2": ("sbuf", [128, 256], "float32"),
+    "XI": ("sbuf", [128, 128], "int32"),
+    "CI": ("sbuf", [128, 128], "int32"),
+    "DD": ("sbuf", [128, 128], "float32"),
+    "LT": ("sbuf", [128, 512], "float32"),
+    "tt": ("sbuf", [128, 512], "float32"),
+    "tm": ("sbuf", [128, 256], "float32"),
+    "tn": ("sbuf", [128, 128], "float32"),
+    "cl": ("sbuf", [128, 128], "float32"),
+    "dc": ("sbuf", [128, 128], "float32"),
+    "Mv": ("sbuf", [128, 128], "float32"),
+    "GO": ("sbuf", [128, 128], "float32"),
+}
+for _i in range(8):
+    SCRATCH["b%d" % _i] = ("psum", [128, 512], "float32")
+EX = ["xQ", "xW", "xB", "xM", "xW1", "xB2", "xM2"]
+SEMAPHORES = ["v", "s", "p", "g", "rl", "dq1", "dgo"] + ["d%d" % i for i in range(9)] + EX
+
+
+def make(g, T):
+    QO = {"v": g.vector, "s": g.scalar, "p": g.tensor, "y": g.sync, "g": g}
+    cnt = {"v": 0, "s": 0, "p": 0, "g": 0}
+    known = {q: {} for q in QO}
+    clk, acc = {}, {}
+
+    def waits(q, toks):
+        k = known[q]
+        todo = {}
+        for ch, n in toks:
+            if k.get(ch, 0) < n:
+                todo[ch] = max(n, todo.get(ch, 0))
+        items = sorted(todo.items())
+        for ch, n in items:
+            if any(c2 != ch and clk[(c2, n2)].get(ch, 0) >= n for c2, n2 in items):
+                continue
+            QO[q].wait_ge(T.sem[ch], n)
+            k[ch] = max(n, k.get(ch, 0))
+            for c3, n3 in clk[(ch, n)].items():
+                k[c3] = max(n3, k.get(c3, 0))
+
+    def is_bank(key):
+        return len(key) == 2 and key[0] == "b" and key[1].isdigit()
+
+    def deps(q, r, w, isdma):
+        toks = set()
+        for lst, wr in ((r, False), (w, True)):
+            for key, lo, hi in lst:
+                bank = is_bank(key)
+                for lo2, hi2, tok, q2, w2 in acc.get(key, []):
+                    same = q2 == q and not isdma
+                    if same and q == "p":
+                        continue
+                    if bank and not same:
+                        toks.add(tok)
+                        continue
+                    if lo2 >= hi or lo >= hi2:
+                        continue
+                    if w2 or (wr and not same):
+                        toks.add(tok)
+        return toks
+
+    def record(q, r, w, tok):
+        for key, lo, hi in w:
+            bank = is_bank(key)
+            acc[key] = [a for a in acc.get(key, []) if not ((lo <= a[0] and a[1] <= hi) or (bank and a[3] != q))]
+            acc[key].append((lo, hi, tok, q, True))
+        for key, lo, hi in r:
+            bank = is_bank(key)
+            acc[key] = [a for a in acc.get(key, [])
+                        if not ((not a[4] and a[3] == q and q in cnt and lo <= a[0] and a[1] <= hi) or (bank and a[3] != q))]
+            acc[key].append((lo, hi, tok, q, False))
+
+    def op(q, fn, r, w):
+        waits(q, deps(q, r, w, False))
+        cnt[q] += 1
+        fn(QO[q]).then_inc(T.sem[q], 1)
+        tok = (q, cnt[q])
+        c = dict(known[q])
+        c[q] = cnt[q]
+        clk[tok] = c
+        record(q, r, w, tok)
+
+    def dma(q, out, in_, r, w, sem, total=16):
+        waits(q, deps(q, r, w, True))
+        QO[q].dma_start(out, in_).then_inc(T.sem[sem], 16)
+        tok = (sem, total)
+        c = dict(known[q])
+        c[sem] = total
+        clk[tok] = c
+        record("d", r, w, tok)
+
+    def arrives(sem, total, w):
+        tok = (sem, total)
+        clk[tok] = {sem: total}
+        record("d", [], w, tok)
+
+    def reads(q, r):
+        waits(q, deps(q, r, [], True))
+
+    def finish(q, toks):
+        for ch in ("v", "s", "p", "g"):
+            if cnt[ch]:
+                toks.append((ch, cnt[ch]))
+        for ch, n in toks:
+            if known[q].get(ch, 0) < n or ch not in cnt:
+                QO[q].wait_ge(T.sem[ch], n)
+                known[q][ch] = n
+
+    return op, dma, arrives, reads, finish
+
+
+def run(*gens):
+    gens = list(gens)
+    while gens:
+        left = []
+        for x in gens:
+            try:
+                next(x)
+                left.append(x)
+            except StopIteration:
+                pass
+        gens = left
+
+
+def rank_program(g, core, T, topo):
+    rank = T.rank_of(core)
+    if rank is None:
+        return
+    op, dma, arrives, reads, finish = make(g, T)
+    own = V * rank
+    others = [c for c in T.cores if c != core]
+    R = range(4)
+
+    def ap(b, lo, hi):
+        return T[b][:, lo:hi]
+
+    def tt(o, a, b, f):
+        op("v", lambda e: e.tensor_tensor(ap(*o), ap(*a), ap(*b), f), [a, b], [o])
+
+    def ts(o, a, s1, s2, f1, f2=None):
+        rd = [a] + [x for x in (s1, s2) if isinstance(x, tuple)]
+        x1 = ap(*s1) if isinstance(s1, tuple) else s1
+        x2 = ap(*s2) if isinstance(s2, tuple) else s2
+        if f2 is None:
+            op("v", lambda e: e.tensor_scalar(ap(*o), ap(*a), x1, x2, f1), rd, [o])
+        else:
+            op("v", lambda e: e.tensor_scalar(ap(*o), ap(*a), x1, x2, f1, f2), rd, [o])
+
+    def cp(q, o, a):
+        if q == "v":
+            op("v", lambda e: e.tensor_copy(ap(*o), ap(*a)), [a], [o])
+        else:
+            op("s", lambda e: e.activation(ap(*o), ap(*a), F.Copy), [a], [o])
+
+    def scaled(o, a, col, bias=None):
+        rd = [a, col] + ([bias] if bias else [])
+        if bias:
+            op("s", lambda e: e.activation(ap(*o), ap(*a), F.Identity, bias=ap(*bias), scale=ap(*col)), rd, [o])
+        else:
+            op("s", lambda e: e.activation(ap(*o), ap(*a), F.Identity, scale=ap(*col)), rd, [o])
+
+    def dcol(d, k, b0, b1):
+        return (d + "#%d" % k, 128 * b0, 128 * b1), T[d][:, 128 * b0 + k:128 * b1:16]
+
+    def mm(o, lt, rh, start, stop, r):
+        op("p", lambda e: e.matmul(ap(*o), lt, rh, start, stop), r, [o])
+
+    def fill(b, lo, hi, x):
+        op("v", lambda e: e.memset(ap(b, lo, hi), x), [], [(b, lo, hi)])
+
+    dma("s", T.nbi[:], T.nb[:], [], [("nbi", 0, 512)], "d8")
+    for i in R:
+        a = 512 * i
+        dma("y", T.Qw[:, 16 + a:16 + a + 512], T.qu[:, a:a + 512], [], [("Qw", 16 + a, 16 + a + 512)], "d%d" % i)
+        dma("s", T.Pb[:, a:a + 512], T.po[:, a:a + 512], [], [("Pb", a, a + 512)], "d%d" % (4 + i))
+
+    msk = topo.mask(core, others[0])
+    for c in others[1:]:
+        msk &= topo.mask(core, c)
+    ne = bin(msk).count("1")
+    sent = [0]
+    arrives("xQ", 3 * ne, [("Qw", 16 + V, 16 + HALO1)])
+    for b, x in (("W", "xW"), ("Bw", "xB"), ("Mw", "xM"), ("M2w", "xM2")):
+        arrives(x, 3 * ne, [(b, V, HALO1)])
+    for b, x in (("W1", "xW1"), ("B2w", "xB2")):
+        arrives(x, 3 * ne, [(b, 16 + V, HALO2)])
+
+    def share(b, sem, lo, w, base):
+        reads("g", [(b, lo, lo + w)])
+        ids, dst = [], []
+        for c in others:
+            q = T.rank_of(c)
+            at = base + w * (rank if rank < q else rank - 1)
+            rid, pid = topo.addr(c)[0], topo.addr(c)[1]
+            ids.append(DstId(rid=rid, pnc=pid))
+            dst.append(T[b][:, at:at + w])
+        g.remote_dma_fused([RemoteDMATransfer(dst_ids=ids, dma_engine_mask=msk, remote_sem=T.sem[sem],
+                                              srcs=[T[b][:, lo:lo + w]], dsts=dst)], local_sem=T.sem.rl)
+        sent[0] += ne
+
+    def g_sel(o, i, pat, c, base, cm):
+        op("g", lambda e: e.affine_select(ap(*o), ap(*i), pat, c, 0.0, base, cm), [i], [o])
+
+    def g_iota(o, pat, base, cm, fl=True, w=None):
+        if fl:
+            op("g", lambda e: e.iota(ap(*o), pat, base, cm, allow_small_or_imprecise_dtypes=True), [], w or [o])
+        else:
+            op("g", lambda e: e.iota(ap(*o), pat, base, cm), [], [o])
+
+    def classes(d):
+        return [(d + "#%d" % k, 0, V) for k in range(16)]
+
+    def ci(k):
+        return ("ci", k, k + 1)
+
+    def cf(k):
+        return ("cf", k, k + 1)
+
+    fill("ON", 0, 512, 1.0)
+    fill("Qw", 0, 16, 0.0)
+    g_iota(ci(0), [[0, 1]], 0, 1, False)
+    g_sel(("E8", 0, 8), ("ON", 0, 8), [[-16, 8]], A.is_ge, 0, 1)
+    g_sel(("E8", 0, 8), ("E8", 0, 8), [[16, 8]], A.is_ge, 15, -1)
+    g_sel(("Id", 0, 128), ("ON", 0, 128), [[-1, 128]], A.is_equal, 0, 1)
+    g_iota(("VC", 0, 128), [[128, 16], [0, 8]], own, 1)
+    for x in range(4):
+        n = CW[x] // 16
+        g_iota(("VT", GB[x] // 16, GB[x] // 16 + 4 * n), [[0, 4], [16, n]], own + C0[x], 0)
+    K1 = {"A": (0, 2, 0), "L": (2, 8, 64), "H": (8, 16, 256)}
+    K2 = {"A": (0, 4, 0), "L": (4, 8, 128), "H": (8, 16, 256)}
+    op("v", lambda e: e.memset(T.DS[:], 0.0), [], classes("DS"))
+    ts(ci(1), ci(0), 15, None, A.bitwise_and)
+    ts(ci(2), ci(1), 2, None, A.logical_shift_right)
+    ts(ci(3), ci(1), 3, None, A.bitwise_and)
+    tt(cf(1), ci(3), ci(2), A.is_lt)
+    tt(cf(2), ci(3), ci(2), A.is_equal)
+    tt(cf(3), ci(3), ci(2), A.is_gt)
+    ts(cf(4), cf(1), -1.0, 1.0, A.mult, A.add)
+    ts(cf(6), cf(3), 2.0, cf(2), A.mult, A.add)
+    ts(cf(5), ci(3), 0.0, cf(1), A.is_equal, A.mult)
+    ts(("wS", 0, 8), ("E8", 0, 8), cf(6), None, A.mult)
+    tt(cf(7), cf(6), cf(5), A.add)
+    scaled(("PM", 0, 128), ("Id", 0, 128), cf(4))
+    ts(("wC", 0, 8), ("E8", 0, 8), cf(7), None, A.mult)
+    scaled(("PMf", 0, 128), ("Id", 0, 128), cf(4))
+    scaled(("PMh", 0, 128), ("Id", 0, 128), cf(4))
+    scaled(("PI", 0, 128), ("Id", 0, 128), cf(1))
+    vc = ("VC", 0, 128)
+    k9, a9 = dcol("DS", 9, 0, 16)
+    k13, a13 = dcol("DS", 13, 0, 16)
+    k14, a14 = dcol("DS", 14, 0, 16)
+    op("v", lambda e: e.tensor_copy(a9, ap(*vc)), [vc], [k9])
+    op("v", lambda e: e.tensor_scalar(a14, ap(*vc), 0.0, 1.0, A.mult, A.add), [vc], [k14])
+    op("v", lambda e: e.tensor_tensor(a13, ap(*vc), a9, A.subtract), [vc, k9], [k13])
+    share("Qw", "xQ", 16, NB, 16 + V)
+
+    def number_to_place(src, n, base0, halo, h):
+        off = [(base0 if k == rank else halo + h * (k if k < rank else k - 1)) - V * k for k in range(N)]
+        st = [k for k in range(1, N) if off[k] != off[k - 1]]
+        ts(("mA", 0, n), src, float(off[0]), None, A.add)
+        for k in st:
+            ts(("mB", 128 * (k - 1), 128 * (k - 1) + n), src, float(V * k), float(off[k] - off[k - 1]), A.is_ge, A.mult)
+        for k in st:
+            tt(("mA", 0, n), ("mA", 0, n), ("mB", 128 * (k - 1), 128 * (k - 1) + n), A.add)
+
+    def nbs(x, s):
+        t0 = 128 * s + C0[x] // 16
+        return ("nbi", t0, t0 + CW[x] // 16)
+
+    def tbl(b, x, s):
+        w, lo = CW[x] // 16, GB[x] // 16
+        return (b, lo + s * w, lo + (s + 1) * w)
+
+    for x in (2, 3, 1):
+        for s in R:
+            ts(tbl("L1", x, s), nbs(x, s), float(-own - (NB if x > 1 else 0)), None, A.add)
+    for s in R:
+        cp("v", ("NF", 16 * s, 16 * s + 16), nbs(0, s))
+    number_to_place(("NF", 0, 64), 64, 0, V, NB)
+    cp("v", ("L1", 0, 64), ("mA", 0, 64))
+    ts(("posq", 0, 64), ("mA", 0, 64), 16.0, None, A.add)
+
+    ts(cf(8), ci(1), 9.0, None, A.is_equal)
+    ts(cf(9), ci(1), 13.0, cf(8), A.is_equal, A.add)
+    for s in R:
+        ts(cf(10 + s), ci(1), 14.0, 8192.0 * (3 - s), A.is_equal, A.mult)
+    for s in R:
+        tt(cf(10 + s), cf(10 + s), cf(9), A.add)
+    for s in R:
+        ts(("wKf", 8 * s, 8 * s + 8), ("E8", 0, 8), cf(10 + s), None, A.mult)
+    cp("v", ("wK", 0, 32), ("wKf", 0, 32))
+    cp("v", cf(0), ci(1))
+
+    def s_sum(bank, blks):
+        for b in blks:
+            src = ("PRS", 128 * b, 128 * b + 128)
+            mm((bank, 8 * b, 8 * b + 8), ap(*src), T.wS[:], True, True, [src, ("wS", 0, 8)])
+
+    def pieces(d, ks, src, b0, b1):
+        rem = ("rem", 8 * b0, 8 * b1)
+        for i, k in enumerate(ks):
+            kk, aa = dcol(d, k, b0, b1)
+            if i == len(ks) - 1:
+                kp, pv = dcol(d, ks[i - 1], b0, b1)
+                op("v", lambda e: e.tensor_tensor(aa, ap(*src), pv, A.subtract), [src, kp], [kk])
+            else:
+                op("v", lambda e: e.tensor_copy(aa, ap(*src)), [src], [kk])
+                yield
+                if i < len(ks) - 2:
+                    op("v", lambda e: e.tensor_tensor(ap(*rem), ap(*src), aa, A.subtract), [src, kk], [rem])
+                    src = rem
+            yield
+
+    def spread(d, ks, win, base, b0, b1, bank, q, with_p=False):
+        o = (bank, 0, 128 * (b1 - b0))
+        if with_p:
+            src = ("Pb", 128 * b0, 128 * b1)
+            mm(o, T.PM[:], ap(*src), True, False, [src, ("PM", 0, 128)])
+        for b in range(b0, b1):
+            mm((bank, 128 * (b - b0), 128 * (b - b0) + 128), T[d][:, 128 * b:128 * b + 128], T.Id[:], not with_p,
+               (b == b1 - 1) or not with_p, [(d + "#%d" % k, 128 * b, 128 * b + 128) for k in ks] + [("Id", 0, 128)])
+        cp(q, (win, base + 128 * b0, base + 128 * b1), o)
+
+    def posq_of(x):
+        for s in R:
+            ts(tbl("posq", x, s), nbs(x, s), float(16 - own), None, A.add)
+
+    DSK = [4, 8, 12, 9, 13, 14]
+    for i in R:
+        q = ("Qw", 16 + 512 * i, 528 + 512 * i)
+        c = ("C1f", 512, 1024) if i == 1 else ("b%d" % i, 0, 512)
+        scaled(c, q, cf(4), cf(1))
+        tt(("PRS", 512 * i, 512 * i + 512), ("Pb", 512 * i, 512 * i + 512), c, A.mult)
+        s_sum("b4" if i < 2 else "b5", range(4 * i, 4 * i + 4))
+        if i == 0:
+            posq_of(1)
+            posq_of(2)
+        if i == 1:
+            run(pieces("DS", [4, 8, 12], ("b4", 0, 64), 0, 8))
+            spread("DS", DSK, "W", 0, 0, 4, "b6", "s", True)
+            spread("DS", DSK, "W", 0, 4, 8, "b7", "v", True)
+            share("W", "xW", 0, NB, V)
+            posq_of(3)
+        if i == 2:
+            ts(("VT", 0, 512), ("VT", 0, 512), cf(0), None, A.add)
+    run(pieces("DS", [4, 8, 12], ("b5", 64, 128), 8, 16))
+    spread("DS", DSK, "W", 0, 8, 12, "b4", "s", True)
+    spread("DS", DSK, "W", 0, 12, 16, "b6", "v", True)
+
+    g_iota(("DB", 0, V), [[0, V]], 0, 0, True, classes("DB"))
+    for nm, K in (("VK1", K1), ("VK2", K2)):
+        for ch in "HLA":
+            b0, b1, o = K[ch]
+            g_iota((nm, o, o + 32 * (b1 - b0)), [[-8192, 4], [128, b1 - b0], [0, 8]], own + 3 * 8192 + 128 * b0, 1)
+        if nm == "VK1":
+            g_iota(("TB", 0, V), [[0, V]], 0, 0)
+            g_iota(("DM", 0, V), [[0, V]], 0, 0, True, classes("DM"))
+
+    def gather(q, out, lo, hi, win, w0, w1, offs):
+        o, wn, of = (out, lo, hi), (win, w0, w1), (offs, lo // 16, hi // 16)
+        if q == "v":
+            op("v", lambda e: e.tensor_copy(ap(*o), ap(*wn).indirect(ap(*of))), [wn, of], [o])
+        else:
+            op("s", lambda e: e.activation(ap(*o), ap(*wn).indirect(ap(*of)), F.Copy), [wn, of], [o])
+
+    def fused(lo, hi, win, w0, w1, offs, c0, c1):
+        o, wn, of, c = ("PR", lo, hi), (win, w0, w1), (offs, lo // 16, hi // 16), ("C1f", c0, c1)
+        op("v", lambda e: e.tensor_tensor(ap(*o), ap(*wn).indirect(ap(*of)), ap(*c), A.mult), [wn, of, c], [o])
+
+    def sums(src, w, x, s, c0, c1, bank, col, n, b0):
+        for b in range(c0 // 128, c1 // 128):
+            lo = GB[x] + s * CW[x] + 128 * b - C0[x]
+            at = col + s * n + 8 * (b - b0)
+            sr = (src, lo, lo + 128)
+            mm((bank, at, at + 8), ap(*sr), ap(*w), True, True, [sr, w])
+
+    def costs(K, ch, x, bank, slots=R):
+        b0, b1, _ = K[ch]
+        for s in slots:
+            for c0 in range(C0[x], C0[x] + CW[x], 512):
+                k, w = c0 // 512, min(512, CW[x])
+                lo = GB[x] + s * CW[x] + c0 - C0[x]
+                tt(("PR", lo, lo + w), ("GA", lo, lo + w), ("b%d" % k, c0 - 512 * k, c0 - 512 * k + w), A.mult)
+                sums("PR", wC, x, s, c0, c0 + w, bank, 0, 8 * (b1 - b0), b0)
+                yield
+
+    def fused_costs(K, ch, x, win, w0, w1, offs, bank):
+        b0, b1, _ = K[ch]
+        for s in R:
+            lo = GB[x] + s * CW[x]
+            fused(lo, lo + CW[x], win, w0, w1, offs, C0[x], C0[x] + CW[x])
+            sums("PR", wC, x, s, C0[x], C0[x] + CW[x], bank, 0, 8 * (b1 - b0), b0)
+            sums("PR", ("wKf", 8 * s, 8 * s + 8), x, s, C0[x], C0[x] + CW[x], bank, 256, 8 * (b1 - b0), b0)
+
+    def numbers(K, ch, x, bank, slots=R):
+        b0, b1, _ = K[ch]
+        for s in slots:
+            sums("GA", ("wK", 8 * s, 8 * s + 8), x, s, C0[x], C0[x] + CW[x], bank, 256, 8 * (b1 - b0), b0)
+
+    def bests(K, ch, x, bank, slots=R):
+        b0, b1, _ = K[ch]
+        for s in slots:
+            sums("GB", E8, x, s, C0[x], C0[x] + CW[x], bank, 0, 8 * (b1 - b0), b0)
+
+    def best_of(K, ch, bank):
+        b0, b1, o = K[ch]
+        n, h = 8 * (b1 - b0), o // 2
+        be = ("best", 8 * b0, 8 * b1)
+        cp("v", ("t1", h, h + 2 * n), (bank, 0, 2 * n))
+        yield
+        tt(("t2", h, h + 2 * n), (bank, 2 * n, 4 * n), ("t1", h, h + 2 * n), A.min)
+        yield
+        tt(be, ("t2", h, h + n), ("t2", h + n, h + 2 * n), A.min)
+        yield
+        yield from pieces("DB", BK, be, b0, b1)
+
+    def choice(K, ch, bank, vk):
+        b0, b1, o = K[ch]
+        n, h = 8 * (b1 - b0), o // 2
+        be = ("best", 8 * b0, 8 * b1)
+        kk = (bank, 256, 256 + 4 * n)
+        for s in R:
+            tt(("E", o + s * n, o + (s + 1) * n), (bank, s * n, (s + 1) * n), be, A.is_equal)
+            yield
+        tt(("LT", o, o + 4 * n), kk, (vk, o, o + 4 * n), A.is_gt)
+        yield
+        tt(("X", o, o + 4 * n), kk, ("E", o, o + 4 * n), A.mult)
+        yield
+        tt(("X2", h, h + 2 * n), ("X", o, o + 2 * n), ("X", o + 2 * n, o + 4 * n), A.max)
+        yield
+        xi, cc = ("XI", 8 * b0, 8 * b1), ("CI", 8 * b0, 8 * b1)
+        tt(xi, ("X2", h, h + n), ("X2", h + n, h + 2 * n), A.max)
+        yield
+        ts(cc, xi, 8191, None, A.bitwise_and)
+        yield
+        tt(("DD", 8 * b0, 8 * b1), cc, ("VC", 8 * b0, 8 * b1), A.subtract)
+        yield
+
+    def move_of(K, ch, bank):
+        b0, b1, o = K[ch]
+        n, h = 8 * (b1 - b0), o // 2
+        c = (8 * b0, 8 * b1)
+        tt(("tt", o, o + 4 * n), (bank, 0, 4 * n), ("LT", o, o + 4 * n), A.add)
+        yield
+        tt(("tm", h, h + 2 * n), ("tt", o, o + 2 * n), ("tt", o + 2 * n, o + 4 * n), A.min)
+        yield
+        tt(("tn",) + c, ("tm", h, h + n), ("tm", h + n, h + 2 * n), A.min)
+        yield
+        tt(("cl",) + c, ("tn",) + c, ("best",) + c, A.is_gt)
+        yield
+        tt(("dc",) + c, ("cl",) + c, ("DD",) + c, A.mult)
+        yield
+        tt(("Mv",) + c, ("dc",) + c, ("VC",) + c, A.add)
+        yield
+        yield from pieces("DM", MK, ("Mv",) + c, b0, b1)
+
+    wC, E8 = ("wC", 0, 8), ("E8", 0, 8)
+    BK, MK = [0, 1, 2], [0, 1]
+
+    gather("s", "GA", GB[3], GB[3] + 2048, "W", NB, V, "L1")
+    gather("s", "GA", GB[3] + 2048, 8192, "W", NB, V, "L1")
+    gather("s", "GA", GB[1], GB[2], "W", 0, V, "L1")
+    gather("s", "GA", 0, GB[1], "W", 0, HALO1, "L1")
+    fused_costs(K1, "L", 2, "W", NB, V, "L1", "b5")
+    run(costs(K1, "H", 3, "b4", (0, 1)))
+    numbers(K1, "H", 3, "b4", (0, 1))
+    run(costs(K1, "H", 3, "b4", (2, 3)))
+    run(costs(K1, "L", 1, "b5"), best_of(K1, "H", "b4"))
+    spread("DB", BK, "Bw", 0, 8, 12, "b6", "s")
+    spread("DB", BK, "Bw", 0, 12, 16, "b7", "s")
+    run(best_of(K1, "L", "b5"), costs(K1, "A", 0, "b3"))
+    spread("DB", BK, "Bw", 0, 4, 8, "b6", "s")
+    spread("DB", BK, "Bw", 0, 2, 4, "b7", "v")
+    numbers(K1, "H", 3, "b4", (2, 3))
+    numbers(K1, "L", 1, "b5")
+    numbers(K1, "A", 0, "b3")
+
+    gather("s", "GB", GB[3], GB[3] + 2048, "Bw", NB, V, "L1")
+    gather("s", "GB", GB[3] + 2048, 8192, "Bw", NB, V, "L1")
+    gather("s", "GB", GB[2], GB[3], "Bw", NB, V, "L1")
+    run(best_of(K1, "A", "b3"), choice(K1, "H", "b4", "VK1"))
+    spread("DB", BK, "Bw", 0, 0, 2, "b6", "v")
+    share("Bw", "xB", 0, NB, V)
+    gather("s", "GB", GB[1], GB[2], "Bw", 0, V, "L1")
+    run(choice(K1, "L", "b5", "VK1"), choice(K1, "A", "b3", "VK1"))
+    bests(K1, "H", 3, "b1")
+    bests(K1, "L", 2, "b2")
+    run(move_of(K1, "H", "b1"))
+    spread("DM", MK, "Mw", 0, 8, 12, "b6", "v")
+    spread("DM", MK, "Mw", 0, 12, 16, "b7", "v")
+    bests(K1, "L", 1, "b2")
+    gather("s", "GB", 0, GB[1], "Bw", 0, HALO1, "L1")
+    for b in range(16):
+        o, a = T.TB[:, 129 * b:128 * b + 128:16], T.E8[:]
+        op("s", lambda e: e.activation(o, a, F.Copy), [E8], [("TB", 128 * b, 128 * b + 128)])
+    run(move_of(K1, "L", "b2"))
+    spread("DM", MK, "Mw", 0, 4, 8, "b6", "s")
+    spread("DM", MK, "Mw", 0, 2, 4, "b7", "v")
+    bests(K1, "A", 0, "b0")
+    run(move_of(K1, "A", "b0"))
+    spread("DM", MK, "Mw", 0, 0, 2, "b6", "v")
+    share("Mw", "xM", 0, NB, V)
+
+    def tables(lo, hi, bank):
+        o = (bank, lo // 16, hi // 16)
+        for b in range(16):
+            l = ("TB", 128 * b, 128 * b + 128)
+            mm(o, ap(*l), T.GA[:, lo + b:hi:16], b == 0, b == 15, [l, ("GA", lo, hi)])
+
+    def start_q1(i):
+        o, a = ("b%d" % i, 0, 512), ("Qw", 16 + 512 * i, 528 + 512 * i)
+        mm(o, T.PMf[:], ap(*a), True, False, [a, ("PMf", 0, 128)])
+        mm(o, T.PI[:], T.ON[:], False, False, [("PI", 0, 128), ("ON", 0, 512)])
+
+    def pull_list(lo, hi, bank):
+        tt(("EQ", lo, hi), (bank, lo, hi), ("VT", lo, hi), A.is_equal)
+        yield
+        tt(("LQ", lo, hi), ("EQ", lo, hi), ("posq", lo, hi), A.mult)
+        yield
+
+    def next_list(lo, hi, bank):
+        ts(("EQ", lo, hi), ("EQ", lo, hi), -BIG, float(16 - own), A.mult, A.add)
+        yield
+        tt(("L2", lo, hi), (bank, lo, hi), ("EQ", lo, hi), A.add)
+        yield
+
+    def pull(x, s, c0, c1, stop):
+        k, lo = c0 // 512, GB[x] + s * CW[x] + c0 - C0[x]
+        a = ("GH", lo, lo + c1 - c0)
+        mm(("b%d" % k, c0 - 512 * k, c1 - 512 * k), T.PMh[:], ap(*a), False, stop, [a, ("PMh", 0, 128)])
+
+    OWN2 = 16 + V
+    gather("s", "GA", GB[3], GB[3] + 2048, "Mw", NB, V, "L1")
+    gather("s", "GA", GB[3] + 2048, 8192, "Mw", NB, V, "L1")
+    gather("v", "GA", GB[2], GB[3], "Mw", NB, V, "L1")
+    gather("v", "GA", GB[1], GB[2], "Mw", 0, V, "L1")
+    start_q1(1)
+    tables(GB[3], GB[3] + 2048, "b4")
+    tables(GB[1], GB[3], "b5")
+    tables(GB[3] + 2048, 8192, "b6")
+    run(pull_list(64, 256, "b5"), pull_list(256, 384, "b4"))
+    gather("s", "GH", GB[2], GB[3], "Qw", 0, OWN2, "LQ")
+    gather("s", "GA", 0, GB[1], "Mw", 0, HALO1, "L1")
+    start_q1(0)
+    tables(0, GB[1], "b7")
+    gather("v", "GH", GB[3], GB[3] + 2048, "Qw", 0, OWN2, "LQ")
+    run(pull_list(384, 512, "b6"), pull_list(0, 64, "b7"))
+    gather("s", "GH", GB[1], GB[2], "Qw", 0, OWN2, "LQ")
+    gather("v", "GH", 0, GB[1], "Qw", 0, 16 + HALO1, "LQ")
+    gather("s", "GH", GB[3] + 2048, 8192, "Qw", 0, OWN2, "LQ")
+    start_q1(2)
+    start_q1(3)
+    for s in R:
+        pull(2, s, 512, 1024, s == 3)
+    for s in R:
+        pull(1, s, 256, 512, False)
+    for s in R:
+        pull(0, s, 0, 256, s == 3)
+    for s in (0, 1):
+        for c in (1024, 1536):
+            pull(3, s, c, c + 512, False)
+    for c in (1024, 1536):
+        for s in (2, 3):
+            pull(3, s, c, c + 512, s == 3)
+    ts(("NF", 0, 64), ("b7", 0, 64), 0.0, None, A.add)
+    ts(("NF", 64, 128), ("b5", 64, 128), 0.0, None, A.add)
+    run(next_list(256, 384, "b4"), next_list(128, 256, "b5"))
+    run(next_list(384, 512, "b6"))
+
+    def q1_out(i):
+        cp("s", ("C1f", 512 * i, 512 * i + 512), ("b%d" % i, 0, 512))
+
+    def own_sum(i, bank):
+        tt(("PRS", 512 * i, 512 * i + 512), ("Pb", 512 * i, 512 * i + 512), ("b%d" % i, 0, 512), A.mult)
+        s_sum(bank, range(4 * i, 4 * i + 4))
+
+    own_sum(1, "b7")
+    own_sum(0, "b7")
+    q1_out(1)
+    q1_out(0)
+    ts(cf(20), ci(1), 4.0, NONE, A.is_equal, A.mult)
+    ts(cf(21), ci(1), 0.0, NONE, A.is_equal, A.mult)
+    ts(("W1", 0, 16), ("ON", 0, 16), cf(20), None, A.mult)
+    ts(("B2w", 0, 16), ("ON", 0, 16), cf(21), None, A.mult)
+    run(pieces("DS", [4, 8, 12], ("b7", 0, 64), 0, 8))
+    spread("DS", DSK, "W1", 16, 0, 4, "b4", "s", True)
+    spread("DS", DSK, "W1", 16, 4, 8, "b6", "v", True)
+    share("W1", "xW1", 16, NC, 16 + V)
+    own_sum(2, "b5")
+    own_sum(3, "b5")
+    number_to_place(("NF", 0, 128), 128, 16, 16 + V, NC)
+    ts(("EQ", 0, 128), ("EQ", 0, 128), -BIG, None, A.mult)
+    run(pieces("DS", [4, 8, 12], ("b5", 64, 128), 8, 16))
+    spread("DS", DSK, "W1", 16, 8, 12, "b7", "s", True)
+    spread("DS", DSK, "W1", 16, 12, 16, "b4", "v", True)
+    tt(("L2", 0, 128), ("mA", 0, 128), ("EQ", 0, 128), A.add)
+    q1_out(2)
+    q1_out(3)
+    for r in range(16):
+        i, j = r // 4, r % 4
+        k = 4 * min(i, j) + max(i, j)
+        dma("y", T.q1[r::16, :], T.C1f[k::16, :], [("C1f", 0, V)], [("q1#%d" % r, 0, V)], "dq1", 16 * (r + 1))
+
+    gather("s", "GA", GB[3], GB[3] + 2048, "W1", 0, OWN2, "L2")
+    gather("s", "GA", 0, GB[2], "W1", 0, HALO2, "L2")
+    gather("s", "GA", GB[3] + 2048, 8192, "W1", 0, OWN2, "L2")
+    fused_costs(K2, "L", 2, "W1", 0, OWN2, "L2", "b6")
+    run(costs(K2, "H", 3, "b4", (0, 1)), best_of(K2, "L", "b6"))
+    spread("DB", BK, "B2w", 16, 4, 8, "b7", "s")
+    numbers(K2, "H", 3, "b4", (0, 1))
+    run(costs(K2, "A", 0, "b5"), costs(K2, "A", 1, "b5"))
+    run(costs(K2, "H", 3, "b4", (2, 3)), best_of(K2, "A", "b5"))
+    spread("DB", BK, "B2w", 16, 0, 4, "b3", "s")
+    share("B2w", "xB2", 16, NC, 16 + V)
+    run(best_of(K2, "H", "b4"), choice(K2, "L", "b6", "VK2"))
+    spread("DB", BK, "B2w", 16, 8, 12, "b7", "s")
+    spread("DB", BK, "B2w", 16, 12, 16, "b3", "v")
+    numbers(K2, "A", 0, "b5")
+    numbers(K2, "A", 1, "b5")
+    numbers(K2, "H", 3, "b4", (2, 3))
+    for b in range(16):
+        l = ("TB", 128 * b, 128 * b + 128)
+        mm(("b2", 0, 128), ap(*l), T.Mw[:, b:V:16], b == 0, b == 15, [l, ("Mw", 0, V)])
+
+    gather("s", "GB", GB[3], GB[3] + 2048, "B2w", 0, OWN2, "L2")
+    gather("s", "GB", GB[3] + 2048, 8192, "B2w", 0, OWN2, "L2")
+    gather("s", "GB", 0, GB[2], "B2w", 0, HALO2, "L2")
+    gather("s", "GB", GB[2], GB[3], "B2w", 0, OWN2, "L2")
+    run(choice(K2, "A", "b5", "VK2"), choice(K2, "H", "b4", "VK2"))
+    number_to_place(("b2", 0, 16), 16, 0, V, NB)
+    cp("v", ("LG", 0, 16), ("mA", 0, 16))
+    ts(("LG", 16, 128), ("b2", 16, 128), float(-own), None, A.add)
+    bests(K2, "H", 3, "b1")
+    run(move_of(K2, "H", "b1"))
+    spread("DM", MK, "M2w", 0, 8, 12, "b7", "v")
+    spread("DM", MK, "M2w", 0, 12, 16, "b3", "v")
+    bests(K2, "A", 0, "b0")
+    bests(K2, "A", 1, "b0")
+    run(move_of(K2, "A", "b0"))
+    spread("DM", MK, "M2w", 0, 0, 4, "b5", "v")
+    share("M2w", "xM2", 0, NB, V)
+    bests(K2, "L", 2, "b2")
+    run(move_of(K2, "L", "b2"))
+    spread("DM", MK, "M2w", 0, 4, 8, "b7", "v")
+
+    gather("s", "GA", 1024, 2048, "M2w", 0, V, "LG")
+    gather("v", "GA", 256, 1024, "M2w", 0, V, "LG")
+    gather("v", "GA", 0, 256, "M2w", 0, HALO1, "LG")
+    order = [8, 9, 10, 11, 12, 13, 14, 15, 2, 3, 4, 5, 6, 7, 0, 1]
+    for b in order:
+        l, a = ("TB", 128 * b, 128 * b + 128), ("GA", 128 * b, 128 * b + 128)
+        mm(("b6", 0, 128), ap(*l), ap(*a), b == order[0], b == order[-1], [l, a])
+    cp("v", ("GO", 0, 128), ("b6", 0, 128))
+    dma("y", T.goal[:], T.GO[:], [("GO", 0, 128)], [("goal", 0, V)], "dgo")
+
+    finish("y", [("dq1", 256), ("dgo", 16)])
+    finish("g", [("rl", sent[0])] + [("d%d" % i, 16) for i in range(9)] + [(x, 3 * ne) for x in EX])

@@ -7,71 +7,23 @@ HALO1, HALO2 = V + 3 * NB, 16 + V + 3 * NC
 BIG = 65536.0
 NONE = float(1 << 24)
 
-SCRATCH = {
-    "Qw": ("sbuf", [128, 16 + HALO1], "float32"),
-    "Pb": ("sbuf", [128, V], "bfloat16"),
-    "nbi": ("sbuf", [128, 512], "int32"),
-    "W": ("sbuf", [128, HALO1], "bfloat16"),
-    "W1": ("sbuf", [128, HALO2], "bfloat16"),
-    "Bw": ("sbuf", [128, HALO1], "bfloat16"),
-    "Mw": ("sbuf", [128, HALO1], "bfloat16"),
-    "B2w": ("sbuf", [128, HALO2], "bfloat16"),
-    "M2w": ("sbuf", [128, HALO1], "bfloat16"),
-    "L1": ("sbuf", [128, 512], "uint16"),
-    "LQ": ("sbuf", [128, 512], "uint16"),
-    "L2": ("sbuf", [128, 512], "uint16"),
-    "LG": ("sbuf", [128, 128], "uint16"),
-    "posq": ("sbuf", [128, 512], "float32"),
-    "VT": ("sbuf", [128, 512], "float32"),
-    "EQ": ("sbuf", [128, 512], "float32"),
-    "NF": ("sbuf", [128, 128], "float32"),
-    "mA": ("sbuf", [128, 128], "float32"),
-    "mB": ("sbuf", [128, 384], "float32"),
-    "GA": ("sbuf", [128, 8192], "bfloat16"),
-    "GB": ("sbuf", [128, 8192], "bfloat16"),
-    "GH": ("sbuf", [128, 8192], "float16"),
-    "PR": ("sbuf", [128, 8192], "float32"),
-    "PRS": ("sbuf", [128, V], "float32"),
-    "C1f": ("sbuf", [128, V], "float32"),
-    "DS": ("sbuf", [128, V], "bfloat16"),
-    "DB": ("sbuf", [128, V], "bfloat16"),
-    "DM": ("sbuf", [128, V], "bfloat16"),
-    "TB": ("sbuf", [128, V], "bfloat16"),
-    "ON": ("sbuf", [128, 512], "bfloat16"),
-    "Id": ("sbuf", [128, 128], "bfloat16"),
-    "PM": ("sbuf", [128, 128], "bfloat16"),
-    "PMh": ("sbuf", [128, 128], "float16"),
-    "PMf": ("sbuf", [128, 128], "float32"),
-    "PI": ("sbuf", [128, 128], "bfloat16"),
-    "E8": ("sbuf", [128, 8], "bfloat16"),
-    "wC": ("sbuf", [128, 8], "float32"),
-    "wS": ("sbuf", [128, 8], "float32"),
-    "wK": ("sbuf", [128, 32], "bfloat16"),
-    "wKf": ("sbuf", [128, 32], "float32"),
-    "ci": ("sbuf", [128, 8], "int32"),
-    "cf": ("sbuf", [128, 32], "float32"),
-    "VC": ("sbuf", [128, 128], "float32"),
-    "VK1": ("sbuf", [128, 512], "float32"),
-    "VK2": ("sbuf", [128, 512], "float32"),
-    "t1": ("sbuf", [128, 256], "float32"),
-    "t2": ("sbuf", [128, 256], "float32"),
-    "best": ("sbuf", [128, 128], "float32"),
-    "rem": ("sbuf", [128, 128], "float32"),
-    "E": ("sbuf", [128, 512], "float32"),
-    "X": ("sbuf", [128, 512], "float32"),
-    "X2": ("sbuf", [128, 256], "float32"),
-    "XI": ("sbuf", [128, 128], "int32"),
-    "CI": ("sbuf", [128, 128], "int32"),
-    "DD": ("sbuf", [128, 128], "float32"),
-    "LT": ("sbuf", [128, 512], "float32"),
-    "tt": ("sbuf", [128, 512], "float32"),
-    "tm": ("sbuf", [128, 256], "float32"),
-    "tn": ("sbuf", [128, 128], "float32"),
-    "cl": ("sbuf", [128, 128], "float32"),
-    "dc": ("sbuf", [128, 128], "float32"),
-    "Mv": ("sbuf", [128, 128], "float32"),
-    "GO": ("sbuf", [128, 128], "float32"),
-}
+SCRATCH = {}
+for _n, _w, _t in (
+        ("Qw", 16 + HALO1, "float32"), ("Pb", V, "bfloat16"), ("nbi", 512, "int32"), ("W", HALO1, "bfloat16"),
+        ("W1", HALO2, "bfloat16"), ("Bw", HALO1, "bfloat16"), ("Mw", HALO1, "bfloat16"), ("B2w", HALO2, "bfloat16"),
+        ("M2w", HALO1, "bfloat16"), ("L1", 512, "uint16"), ("LQ", 512, "uint16"), ("L2", 512, "uint16"), ("LG", 128, "uint16"),
+        ("posq", 512, "float32"), ("VT", 512, "float32"), ("EQ", 512, "float32"), ("NF", 128, "float32"), ("mA", 128, "float32"),
+        ("mB", 384, "float32"), ("GA", 8192, "bfloat16"), ("GB", 8192, "bfloat16"), ("GH", 8192, "float16"),
+        ("PR", 8192, "float32"), ("PRS", V, "float32"), ("C1f", V, "float32"), ("DS", V, "bfloat16"), ("DB", V, "bfloat16"),
+        ("DM", V, "bfloat16"), ("TB", V, "bfloat16"), ("ON", 512, "bfloat16"), ("Id", 128, "bfloat16"), ("PM", 128, "bfloat16"),
+        ("PMh", 128, "float16"), ("PMf", 128, "float32"), ("PI", 128, "bfloat16"), ("E8", 8, "bfloat16"), ("wC", 8, "float32"),
+        ("wS", 8, "float32"), ("wK", 32, "bfloat16"), ("wKf", 32, "float32"), ("ci", 8, "int32"), ("cf", 32, "float32"),
+        ("VC", 128, "float32"), ("VK1", 512, "float32"), ("VK2", 512, "float32"), ("t1", 256, "float32"), ("t2", 256, "float32"),
+        ("best", 128, "float32"), ("rem", 128, "float32"), ("E", 512, "float32"), ("X", 512, "float32"), ("X2", 256, "float32"),
+        ("XI", 128, "int32"), ("CI", 128, "int32"), ("DD", 128, "float32"), ("Dh", 128, "bfloat16"), ("Dl", 128, "float32"),
+        ("LT", 512, "float32"), ("tt", 512, "float32"), ("tm", 256, "float32"), ("tn", 128, "float32"), ("cl", 128, "float32"),
+        ("GO", 128, "float32")):
+    SCRATCH[_n] = ("sbuf", [128, _w], _t)
 for _i in range(8):
     SCRATCH["b%d" % _i] = ("psum", [128, 512], "float32")
 EX = ["xQ", "xW", "xB", "xM", "xW1", "xB2", "xM2"]
@@ -229,11 +181,12 @@ def rank_program(g, core, T, topo):
     def fill(b, lo, hi, x):
         op("v", lambda e: e.memset(ap(b, lo, hi), x), [], [(b, lo, hi)])
 
-    dma("s", T.nbi[:], T.nb[:], [], [("nbi", 0, 512)], "d8")
     for i in R:
         a = 512 * i
         dma("y", T.Qw[:, 16 + a:16 + a + 512], T.qu[:, a:a + 512], [], [("Qw", 16 + a, 16 + a + 512)], "d%d" % i)
         dma("s", T.Pb[:, a:a + 512], T.po[:, a:a + 512], [], [("Pb", a, a + 512)], "d%d" % (4 + i))
+        if i == 0:
+            dma("s", T.nbi[:], T.nb[:], [], [("nbi", 0, 512)], "d8")
 
     msk = topo.mask(core, others[0])
     for c in others[1:]:
@@ -280,32 +233,49 @@ def rank_program(g, core, T, topo):
     fill("ON", 0, 512, 1.0)
     fill("Qw", 0, 16, 0.0)
     g_iota(ci(0), [[0, 1]], 0, 1, False)
+    g_sel(("Id", 0, 128), ("ON", 0, 128), [[-1, 128]], A.is_equal, 0, 1)
     g_sel(("E8", 0, 8), ("ON", 0, 8), [[-16, 8]], A.is_ge, 0, 1)
     g_sel(("E8", 0, 8), ("E8", 0, 8), [[16, 8]], A.is_ge, 15, -1)
-    g_sel(("Id", 0, 128), ("ON", 0, 128), [[-1, 128]], A.is_equal, 0, 1)
     g_iota(("VC", 0, 128), [[128, 16], [0, 8]], own, 1)
     for x in range(4):
         n = CW[x] // 16
         g_iota(("VT", GB[x] // 16, GB[x] // 16 + 4 * n), [[0, 4], [16, n]], own + C0[x], 0)
+    share("Qw", "xQ", 16, NB, 16 + V)
     K1 = {"A": (0, 2, 0), "L": (2, 8, 64), "H": (8, 16, 256)}
     K2 = {"A": (0, 4, 0), "L": (4, 8, 128), "H": (8, 16, 256)}
-    op("v", lambda e: e.memset(T.DS[:], 0.0), [], classes("DS"))
     ts(ci(1), ci(0), 15, None, A.bitwise_and)
+    op("v", lambda e: e.memset(T.DS[:], 0.0), [], classes("DS"))
     ts(ci(2), ci(1), 2, None, A.logical_shift_right)
     ts(ci(3), ci(1), 3, None, A.bitwise_and)
+    cp("v", cf(0), ci(1))
     tt(cf(1), ci(3), ci(2), A.is_lt)
-    tt(cf(2), ci(3), ci(2), A.is_equal)
     tt(cf(3), ci(3), ci(2), A.is_gt)
+    tt(cf(2), ci(3), ci(2), A.is_equal)
     ts(cf(4), cf(1), -1.0, 1.0, A.mult, A.add)
-    ts(cf(6), cf(3), 2.0, cf(2), A.mult, A.add)
     ts(cf(5), ci(3), 0.0, cf(1), A.is_equal, A.mult)
-    ts(("wS", 0, 8), ("E8", 0, 8), cf(6), None, A.mult)
+    ts(cf(6), cf(3), 2.0, cf(2), A.mult, A.add)
+    ts(cf(8), ci(1), 9.0, None, A.is_equal)
     tt(cf(7), cf(6), cf(5), A.add)
+    ts(cf(9), ci(1), 13.0, cf(8), A.is_equal, A.add)
+    for s in R:
+        ts(cf(10 + s), ci(1), 14.0, 8192.0 * (3 - s), A.is_equal, A.mult)
+    for s in R:
+        tt(cf(10 + s), cf(10 + s), cf(9), A.add)
+    ts(cf(20), ci(1), 4.0, NONE, A.is_equal, A.mult)
+    ts(cf(21), ci(1), 0.0, NONE, A.is_equal, A.mult)
     scaled(("PM", 0, 128), ("Id", 0, 128), cf(4))
-    ts(("wC", 0, 8), ("E8", 0, 8), cf(7), None, A.mult)
+    scaled(("wS", 0, 8), ("E8", 0, 8), cf(6))
+    scaled(("wC", 0, 8), ("E8", 0, 8), cf(7))
+    for s in R:
+        scaled(("wKf", 8 * s, 8 * s + 8), ("E8", 0, 8), cf(10 + s))
+    cp("s", ("wK", 0, 32), ("wKf", 0, 32))
     scaled(("PMf", 0, 128), ("Id", 0, 128), cf(4))
     scaled(("PMh", 0, 128), ("Id", 0, 128), cf(4))
     scaled(("PI", 0, 128), ("Id", 0, 128), cf(1))
+    scaled(("W1", 0, 16), ("ON", 0, 16), cf(20))
+    scaled(("B2w", 0, 16), ("ON", 0, 16), cf(21))
+    vt = ("VT", 0, 512)
+    op("s", lambda e: e.activation(ap(*vt), ap(*vt), F.Identity, bias=ap(*cf(0))), [vt, cf(0)], [vt])
     vc = ("VC", 0, 128)
     k9, a9 = dcol("DS", 9, 0, 16)
     k13, a13 = dcol("DS", 13, 0, 16)
@@ -313,7 +283,6 @@ def rank_program(g, core, T, topo):
     op("v", lambda e: e.tensor_copy(a9, ap(*vc)), [vc], [k9])
     op("v", lambda e: e.tensor_scalar(a14, ap(*vc), 0.0, 1.0, A.mult, A.add), [vc], [k14])
     op("v", lambda e: e.tensor_tensor(a13, ap(*vc), a9, A.subtract), [vc, k9], [k13])
-    share("Qw", "xQ", 16, NB, 16 + V)
 
     def number_to_place(src, n, base0, halo, h):
         off = [(base0 if k == rank else halo + h * (k if k < rank else k - 1)) - V * k for k in range(N)]
@@ -324,33 +293,10 @@ def rank_program(g, core, T, topo):
         for k in st:
             tt(("mA", 0, n), ("mA", 0, n), ("mB", 128 * (k - 1), 128 * (k - 1) + n), A.add)
 
-    def nbs(x, s):
-        t0 = 128 * s + C0[x] // 16
-        return ("nbi", t0, t0 + CW[x] // 16)
-
-    def tbl(b, x, s):
-        w, lo = CW[x] // 16, GB[x] // 16
-        return (b, lo + s * w, lo + (s + 1) * w)
-
-    for x in (2, 3, 1):
-        for s in R:
-            ts(tbl("L1", x, s), nbs(x, s), float(-own - (NB if x > 1 else 0)), None, A.add)
-    for s in R:
-        cp("v", ("NF", 16 * s, 16 * s + 16), nbs(0, s))
-    number_to_place(("NF", 0, 64), 64, 0, V, NB)
-    cp("v", ("L1", 0, 64), ("mA", 0, 64))
-    ts(("posq", 0, 64), ("mA", 0, 64), 16.0, None, A.add)
-
-    ts(cf(8), ci(1), 9.0, None, A.is_equal)
-    ts(cf(9), ci(1), 13.0, cf(8), A.is_equal, A.add)
-    for s in R:
-        ts(cf(10 + s), ci(1), 14.0, 8192.0 * (3 - s), A.is_equal, A.mult)
-    for s in R:
-        tt(cf(10 + s), cf(10 + s), cf(9), A.add)
-    for s in R:
-        ts(("wKf", 8 * s, 8 * s + 8), ("E8", 0, 8), cf(10 + s), None, A.mult)
-    cp("v", ("wK", 0, 32), ("wKf", 0, 32))
-    cp("v", cf(0), ci(1))
+    def own_place(x, s):
+        t0, w, lo = 128 * s + C0[x] // 16, CW[x] // 16, GB[x] // 16
+        a, o = ("EQ", t0, t0 + w), ("posq", lo + s * w, lo + (s + 1) * w)
+        op("s", lambda e: e.activation(ap(*o), ap(*a), F.Identity, bias=float(16 - own)), [a], [o])
 
     def s_sum(bank, blks):
         for b in blks:
@@ -372,41 +318,48 @@ def rank_program(g, core, T, topo):
                     src = rem
             yield
 
+    def points(b0, b1, bank):
+        src = ("Pb", 128 * b0, 128 * b1)
+        mm((bank, 0, 128 * (b1 - b0)), T.PM[:], ap(*src), True, False, [src, ("PM", 0, 128)])
+
     def spread(d, ks, win, base, b0, b1, bank, q, with_p=False):
         o = (bank, 0, 128 * (b1 - b0))
-        if with_p:
-            src = ("Pb", 128 * b0, 128 * b1)
-            mm(o, T.PM[:], ap(*src), True, False, [src, ("PM", 0, 128)])
         for b in range(b0, b1):
             mm((bank, 128 * (b - b0), 128 * (b - b0) + 128), T[d][:, 128 * b:128 * b + 128], T.Id[:], not with_p,
                (b == b1 - 1) or not with_p, [(d + "#%d" % k, 128 * b, 128 * b + 128) for k in ks] + [("Id", 0, 128)])
         cp(q, (win, base + 128 * b0, base + 128 * b1), o)
 
-    def posq_of(x):
-        for s in R:
-            ts(tbl("posq", x, s), nbs(x, s), float(16 - own), None, A.add)
-
-    DSK = [4, 8, 12, 9, 13, 14]
+    DSK, SK = [4, 8, 12, 9, 13, 14], [4, 8, 12]
     for i in R:
         q = ("Qw", 16 + 512 * i, 528 + 512 * i)
         c = ("C1f", 512, 1024) if i == 1 else ("b%d" % i, 0, 512)
         scaled(c, q, cf(4), cf(1))
         tt(("PRS", 512 * i, 512 * i + 512), ("Pb", 512 * i, 512 * i + 512), c, A.mult)
-        s_sum("b4" if i < 2 else "b5", range(4 * i, 4 * i + 4))
+        s_sum(("b4", "b4", "b5", "b5")[i], range(4 * i, 4 * i + 4))
         if i == 0:
-            posq_of(1)
-            posq_of(2)
+            cp("v", ("EQ", 0, 512), ("nbi", 0, 512))
         if i == 1:
-            run(pieces("DS", [4, 8, 12], ("b4", 0, 64), 0, 8))
+            for x in (1, 2, 3):
+                for s in R:
+                    own_place(x, s)
+            for s in R:
+                cp("s", ("NF", 16 * s, 16 * s + 16), ("EQ", 128 * s, 128 * s + 16))
+            points(0, 4, "b6")
+            points(4, 8, "b7")
+            run(pieces("DS", SK, ("b4", 0, 64), 0, 8))
             spread("DS", DSK, "W", 0, 0, 4, "b6", "s", True)
             spread("DS", DSK, "W", 0, 4, 8, "b7", "v", True)
             share("W", "xW", 0, NB, V)
-            posq_of(3)
-        if i == 2:
-            ts(("VT", 0, 512), ("VT", 0, 512), cf(0), None, A.add)
-    run(pieces("DS", [4, 8, 12], ("b5", 64, 128), 8, 16))
+    points(8, 12, "b4")
+    points(12, 16, "b6")
+    number_to_place(("NF", 0, 64), 64, 0, V, NB)
+    run(pieces("DS", SK, ("b5", 64, 128), 8, 16))
+    ts(("L1", 128, 512), ("posq", 128, 512), float(-16 - NB), None, A.add)
+    ts(("L1", 64, 128), ("posq", 64, 128), -16.0, None, A.add)
+    cp("v", ("L1", 0, 64), ("mA", 0, 64))
     spread("DS", DSK, "W", 0, 8, 12, "b4", "s", True)
     spread("DS", DSK, "W", 0, 12, 16, "b6", "v", True)
+    ts(("posq", 0, 64), ("mA", 0, 64), 16.0, None, A.add)
 
     g_iota(("DB", 0, V), [[0, V]], 0, 0, True, classes("DB"))
     for nm, K in (("VK1", K1), ("VK2", K2)):
@@ -435,53 +388,60 @@ def rank_program(g, core, T, topo):
             sr = (src, lo, lo + 128)
             mm((bank, at, at + 8), ap(*sr), ap(*w), True, True, [sr, w])
 
-    def costs(K, ch, x, bank, slots=R):
+    def costs(K, ch, x, banks, slots=R):
         b0, b1, _ = K[ch]
         for s in slots:
             for c0 in range(C0[x], C0[x] + CW[x], 512):
                 k, w = c0 // 512, min(512, CW[x])
                 lo = GB[x] + s * CW[x] + c0 - C0[x]
                 tt(("PR", lo, lo + w), ("GA", lo, lo + w), ("b%d" % k, c0 - 512 * k, c0 - 512 * k + w), A.mult)
-                sums("PR", wC, x, s, c0, c0 + w, bank, 0, 8 * (b1 - b0), b0)
+                sums("PR", wC, x, s, c0, c0 + w, banks[s // 2], 0, 8 * (b1 - b0), b0)
                 yield
 
-    def fused_costs(K, ch, x, win, w0, w1, offs, bank):
+    def fused_costs(K, ch, x, win, w0, w1, offs, banks):
         b0, b1, _ = K[ch]
         for s in R:
             lo = GB[x] + s * CW[x]
             fused(lo, lo + CW[x], win, w0, w1, offs, C0[x], C0[x] + CW[x])
-            sums("PR", wC, x, s, C0[x], C0[x] + CW[x], bank, 0, 8 * (b1 - b0), b0)
-            sums("PR", ("wKf", 8 * s, 8 * s + 8), x, s, C0[x], C0[x] + CW[x], bank, 256, 8 * (b1 - b0), b0)
+            sums("PR", wC, x, s, C0[x], C0[x] + CW[x], banks[s // 2], 0, 8 * (b1 - b0), b0)
+            sums("PR", ("wKf", 8 * s, 8 * s + 8), x, s, C0[x], C0[x] + CW[x], banks[0], 256, 8 * (b1 - b0), b0)
 
-    def numbers(K, ch, x, bank, slots=R):
+    def numbers(K, ch, x, banks):
         b0, b1, _ = K[ch]
-        for s in slots:
-            sums("GA", ("wK", 8 * s, 8 * s + 8), x, s, C0[x], C0[x] + CW[x], bank, 256, 8 * (b1 - b0), b0)
+        for s in R:
+            sums("GA", ("wK", 8 * s, 8 * s + 8), x, s, C0[x], C0[x] + CW[x], banks[0], 256, 8 * (b1 - b0), b0)
 
-    def bests(K, ch, x, bank, slots=R):
+    def bests(K, ch, x, bank):
         b0, b1, _ = K[ch]
-        for s in slots:
+        for s in R:
             sums("GB", E8, x, s, C0[x], C0[x] + CW[x], bank, 0, 8 * (b1 - b0), b0)
 
-    def best_of(K, ch, bank):
+    def first_half(K, ch, banks):
+        b0, b1, o = K[ch]
+        n, h = 8 * (b1 - b0), o // 2
+        cp("v", ("t1", h, h + 2 * n), (banks[0], 0, 2 * n))
+
+    def best_of(K, ch, banks, half_done=False):
         b0, b1, o = K[ch]
         n, h = 8 * (b1 - b0), o // 2
         be = ("best", 8 * b0, 8 * b1)
-        cp("v", ("t1", h, h + 2 * n), (bank, 0, 2 * n))
-        yield
-        tt(("t2", h, h + 2 * n), (bank, 2 * n, 4 * n), ("t1", h, h + 2 * n), A.min)
+        if not half_done:
+            first_half(K, ch, banks)
+            yield
+        tt(("t2", h, h + 2 * n), (banks[1], 2 * n, 4 * n), ("t1", h, h + 2 * n), A.min)
         yield
         tt(be, ("t2", h, h + n), ("t2", h + n, h + 2 * n), A.min)
         yield
         yield from pieces("DB", BK, be, b0, b1)
 
-    def choice(K, ch, bank, vk):
+    def choice(K, ch, banks, vk):
         b0, b1, o = K[ch]
         n, h = 8 * (b1 - b0), o // 2
-        be = ("best", 8 * b0, 8 * b1)
-        kk = (bank, 256, 256 + 4 * n)
+        c = (8 * b0, 8 * b1)
+        be = ("best",) + c
+        kk = (banks[0], 256, 256 + 4 * n)
         for s in R:
-            tt(("E", o + s * n, o + (s + 1) * n), (bank, s * n, (s + 1) * n), be, A.is_equal)
+            tt(("E", o + s * n, o + (s + 1) * n), (banks[s // 2], s * n, (s + 1) * n), be, A.is_equal)
             yield
         tt(("LT", o, o + 4 * n), kk, (vk, o, o + 4 * n), A.is_gt)
         yield
@@ -489,12 +449,15 @@ def rank_program(g, core, T, topo):
         yield
         tt(("X2", h, h + 2 * n), ("X", o, o + 2 * n), ("X", o + 2 * n, o + 4 * n), A.max)
         yield
-        xi, cc = ("XI", 8 * b0, 8 * b1), ("CI", 8 * b0, 8 * b1)
-        tt(xi, ("X2", h, h + n), ("X2", h + n, h + 2 * n), A.max)
+        tt(("XI",) + c, ("X2", h, h + n), ("X2", h + n, h + 2 * n), A.max)
         yield
-        ts(cc, xi, 8191, None, A.bitwise_and)
+        ts(("CI",) + c, ("XI",) + c, 8191, None, A.bitwise_and)
         yield
-        tt(("DD", 8 * b0, 8 * b1), cc, ("VC", 8 * b0, 8 * b1), A.subtract)
+        tt(("DD",) + c, ("CI",) + c, ("VC",) + c, A.subtract)
+        yield
+        cp("v", ("Dh",) + c, ("DD",) + c)
+        yield
+        tt(("Dl",) + c, ("DD",) + c, ("Dh",) + c, A.subtract)
         yield
 
     def move_of(K, ch, bank):
@@ -509,57 +472,73 @@ def rank_program(g, core, T, topo):
         yield
         tt(("cl",) + c, ("tn",) + c, ("best",) + c, A.is_gt)
         yield
-        tt(("dc",) + c, ("cl",) + c, ("DD",) + c, A.mult)
-        yield
-        tt(("Mv",) + c, ("dc",) + c, ("VC",) + c, A.add)
-        yield
-        yield from pieces("DM", MK, ("Mv",) + c, b0, b1)
+        for k, d in ((0, "Dh"), (1, "Dl")):
+            kk, aa = dcol("DM", k, b0, b1)
+            op("v", lambda e: e.tensor_tensor(aa, ap(*(("cl",) + c)), ap(*((d,) + c)), A.mult), [("cl",) + c, (d,) + c], [kk])
+            yield
+
+    def start_q1(i):
+        o, a = ("b%d" % i, 0, 512), ("Qw", 16 + 512 * i, 528 + 512 * i)
+        mm(o, T.PMf[:], ap(*a), True, False, [a, ("PMf", 0, 128)])
+        mm(o, T.PI[:], T.ON[:], False, False, [("PI", 0, 128), ("ON", 0, 512)])
+
+    def weights_of_tables():
+        for b in range(16):
+            o, a = T.TB[:, 129 * b:128 * b + 128:16], T.E8[:]
+            op("s", lambda e: e.activation(o, a, F.Copy), [E8], [("TB", 128 * b, 128 * b + 128)])
 
     wC, E8 = ("wC", 0, 8), ("E8", 0, 8)
-    BK, MK = [0, 1, 2], [0, 1]
+    BK, MK = [0, 1, 2], [0, 1, 2, 3]
 
+    bH, bL, bA = ("b4", "b1"), ("b5", "b5"), ("b3", "b3")
     gather("s", "GA", GB[3], GB[3] + 2048, "W", NB, V, "L1")
-    gather("s", "GA", GB[3] + 2048, 8192, "W", NB, V, "L1")
     gather("s", "GA", GB[1], GB[2], "W", 0, V, "L1")
+    gather("s", "GA", GB[3] + 2048, 8192, "W", NB, V, "L1")
     gather("s", "GA", 0, GB[1], "W", 0, HALO1, "L1")
-    fused_costs(K1, "L", 2, "W", NB, V, "L1", "b5")
-    run(costs(K1, "H", 3, "b4", (0, 1)))
-    numbers(K1, "H", 3, "b4", (0, 1))
-    run(costs(K1, "H", 3, "b4", (2, 3)))
-    run(costs(K1, "L", 1, "b5"), best_of(K1, "H", "b4"))
-    spread("DB", BK, "Bw", 0, 8, 12, "b6", "s")
-    spread("DB", BK, "Bw", 0, 12, 16, "b7", "s")
-    run(best_of(K1, "L", "b5"), costs(K1, "A", 0, "b3"))
+    weights_of_tables()
+    fused_costs(K1, "L", 2, "W", NB, V, "L1", bL)
+    run(costs(K1, "H", 3, bH, (0, 1)))
+    run(costs(K1, "L", 1, bL))
+    first_half(K1, "H", bH)
+    run(costs(K1, "H", 3, bH, (2, 3)), best_of(K1, "L", bL))
     spread("DB", BK, "Bw", 0, 4, 8, "b6", "s")
-    spread("DB", BK, "Bw", 0, 2, 4, "b7", "v")
-    numbers(K1, "H", 3, "b4", (2, 3))
-    numbers(K1, "L", 1, "b5")
-    numbers(K1, "A", 0, "b3")
+    spread("DB", BK, "Bw", 0, 2, 4, "b7", "s")
+    numbers(K1, "L", 1, bL)
+    run(best_of(K1, "H", bH, True))
+    spread("DB", BK, "Bw", 0, 8, 12, "b6", "s")
+    spread("DB", BK, "Bw", 0, 12, 16, "b7", "v")
+    run(costs(K1, "A", 0, bA))
 
     gather("s", "GB", GB[3], GB[3] + 2048, "Bw", NB, V, "L1")
     gather("s", "GB", GB[3] + 2048, 8192, "Bw", NB, V, "L1")
     gather("s", "GB", GB[2], GB[3], "Bw", NB, V, "L1")
-    run(best_of(K1, "A", "b3"), choice(K1, "H", "b4", "VK1"))
+    run(best_of(K1, "A", bA))
+    numbers(K1, "H", 3, bH)
+    numbers(K1, "A", 0, bA)
     spread("DB", BK, "Bw", 0, 0, 2, "b6", "v")
     share("Bw", "xB", 0, NB, V)
+    for k, j in ((2, 9), (3, 13)):
+        kk, aa = dcol("DM", k, 0, 16)
+        ks, sv = dcol("DS", j, 0, 16)
+        op("v", lambda e: e.tensor_copy(aa, sv), [ks], [kk])
     gather("s", "GB", GB[1], GB[2], "Bw", 0, V, "L1")
-    run(choice(K1, "L", "b5", "VK1"), choice(K1, "A", "b3", "VK1"))
-    bests(K1, "H", 3, "b1")
-    bests(K1, "L", 2, "b2")
-    run(move_of(K1, "H", "b1"))
+    run(choice(K1, "H", bH, "VK1"), choice(K1, "L", bL, "VK1"))
+    bests(K1, "H", 3, "b2")
+    bests(K1, "L", 2, "b0")
+    run(move_of(K1, "H", "b2"), choice(K1, "A", bA, "VK1"))
     spread("DM", MK, "Mw", 0, 8, 12, "b6", "v")
     spread("DM", MK, "Mw", 0, 12, 16, "b7", "v")
-    bests(K1, "L", 1, "b2")
+    start_q1(2)
+    bests(K1, "L", 1, "b0")
     gather("s", "GB", 0, GB[1], "Bw", 0, HALO1, "L1")
-    for b in range(16):
-        o, a = T.TB[:, 129 * b:128 * b + 128:16], T.E8[:]
-        op("s", lambda e: e.activation(o, a, F.Copy), [E8], [("TB", 128 * b, 128 * b + 128)])
-    run(move_of(K1, "L", "b2"))
+    bests(K1, "A", 0, "b1")
+    run(move_of(K1, "L", "b0"))
     spread("DM", MK, "Mw", 0, 4, 8, "b6", "s")
     spread("DM", MK, "Mw", 0, 2, 4, "b7", "v")
-    bests(K1, "A", 0, "b0")
-    run(move_of(K1, "A", "b0"))
+    run(move_of(K1, "A", "b1"))
     spread("DM", MK, "Mw", 0, 0, 2, "b6", "v")
+    for i in (3, 0, 1):
+        start_q1(i)
     share("Mw", "xM", 0, NB, V)
 
     def tables(lo, hi, bank):
@@ -567,11 +546,6 @@ def rank_program(g, core, T, topo):
         for b in range(16):
             l = ("TB", 128 * b, 128 * b + 128)
             mm(o, ap(*l), T.GA[:, lo + b:hi:16], b == 0, b == 15, [l, ("GA", lo, hi)])
-
-    def start_q1(i):
-        o, a = ("b%d" % i, 0, 512), ("Qw", 16 + 512 * i, 528 + 512 * i)
-        mm(o, T.PMf[:], ap(*a), True, False, [a, ("PMf", 0, 128)])
-        mm(o, T.PI[:], T.ON[:], False, False, [("PI", 0, 128), ("ON", 0, 512)])
 
     def pull_list(lo, hi, bank):
         tt(("EQ", lo, hi), (bank, lo, hi), ("VT", lo, hi), A.is_equal)
@@ -590,44 +564,6 @@ def rank_program(g, core, T, topo):
         a = ("GH", lo, lo + c1 - c0)
         mm(("b%d" % k, c0 - 512 * k, c1 - 512 * k), T.PMh[:], ap(*a), False, stop, [a, ("PMh", 0, 128)])
 
-    OWN2 = 16 + V
-    gather("s", "GA", GB[3], GB[3] + 2048, "Mw", NB, V, "L1")
-    gather("s", "GA", GB[3] + 2048, 8192, "Mw", NB, V, "L1")
-    gather("v", "GA", GB[2], GB[3], "Mw", NB, V, "L1")
-    gather("v", "GA", GB[1], GB[2], "Mw", 0, V, "L1")
-    start_q1(1)
-    tables(GB[3], GB[3] + 2048, "b4")
-    tables(GB[1], GB[3], "b5")
-    tables(GB[3] + 2048, 8192, "b6")
-    run(pull_list(64, 256, "b5"), pull_list(256, 384, "b4"))
-    gather("s", "GH", GB[2], GB[3], "Qw", 0, OWN2, "LQ")
-    gather("s", "GA", 0, GB[1], "Mw", 0, HALO1, "L1")
-    start_q1(0)
-    tables(0, GB[1], "b7")
-    gather("v", "GH", GB[3], GB[3] + 2048, "Qw", 0, OWN2, "LQ")
-    run(pull_list(384, 512, "b6"), pull_list(0, 64, "b7"))
-    gather("s", "GH", GB[1], GB[2], "Qw", 0, OWN2, "LQ")
-    gather("v", "GH", 0, GB[1], "Qw", 0, 16 + HALO1, "LQ")
-    gather("s", "GH", GB[3] + 2048, 8192, "Qw", 0, OWN2, "LQ")
-    start_q1(2)
-    start_q1(3)
-    for s in R:
-        pull(2, s, 512, 1024, s == 3)
-    for s in R:
-        pull(1, s, 256, 512, False)
-    for s in R:
-        pull(0, s, 0, 256, s == 3)
-    for s in (0, 1):
-        for c in (1024, 1536):
-            pull(3, s, c, c + 512, False)
-    for c in (1024, 1536):
-        for s in (2, 3):
-            pull(3, s, c, c + 512, s == 3)
-    ts(("NF", 0, 64), ("b7", 0, 64), 0.0, None, A.add)
-    ts(("NF", 64, 128), ("b5", 64, 128), 0.0, None, A.add)
-    run(next_list(256, 384, "b4"), next_list(128, 256, "b5"))
-    run(next_list(384, 512, "b6"))
-
     def q1_out(i):
         cp("s", ("C1f", 512 * i, 512 * i + 512), ("b%d" % i, 0, 512))
 
@@ -635,74 +571,116 @@ def rank_program(g, core, T, topo):
         tt(("PRS", 512 * i, 512 * i + 512), ("Pb", 512 * i, 512 * i + 512), ("b%d" % i, 0, 512), A.mult)
         s_sum(bank, range(4 * i, 4 * i + 4))
 
+    OWN2 = 16 + V
+    gather("s", "GA", GB[3], GB[3] + 2048, "Mw", NB, V, "L1")
+    gather("s", "GA", GB[3] + 2048, 8192, "Mw", NB, V, "L1")
+    gather("s", "GA", 0, GB[1], "Mw", 0, HALO1, "L1")
+    gather("v", "GA", GB[2], GB[3], "Mw", NB, V, "L1")
+    gather("v", "GA", GB[1], GB[2], "Mw", 0, V, "L1")
+    tables(GB[2], GB[3], "b5")
+    tables(GB[3], GB[3] + 2048, "b4")
+    tables(GB[1], GB[2], "b7")
+    tables(GB[3] + 2048, 8192, "b6")
+    run(pull_list(128, 256, "b5"))
+    run(pull_list(256, 384, "b4"))
+    run(pull_list(64, 128, "b7"))
+    gather("s", "GH", GB[2], GB[3], "Qw", 0, OWN2, "LQ")
+    gather("v", "GH", GB[3], GB[3] + 2048, "Qw", 0, OWN2, "LQ")
+    tables(0, GB[1], "b7")
+    run(pull_list(384, 512, "b6"), pull_list(0, 64, "b7"))
+    gather("s", "GH", GB[1], GB[2], "Qw", 0, OWN2, "LQ")
+    gather("v", "GH", 0, GB[1], "Qw", 0, 16 + HALO1, "LQ")
+    run(next_list(384, 512, "b6"), next_list(128, 256, "b5"))
+    run(next_list(256, 384, "b4"))
+    cp("v", ("NF", 0, 128), ("b7", 0, 128))
+    for c in (0, 512):
+        for s in (2, 3):
+            lo = GB[3] + 1024 * s + c
+            gather("s", "GH", lo, lo + 512, "Qw", 0, OWN2, "LQ")
+    for s in R:
+        pull(2, s, 512, 1024, s == 3)
+    for s in (0, 1):
+        for c in (1024, 1536):
+            pull(3, s, c, c + 512, False)
+    for s in R:
+        pull(1, s, 256, 512, False)
+    for s in R:
+        pull(0, s, 0, 256, s == 3)
+
+    for s in (2, 3):
+        pull(3, s, 1024, 1536, s == 3)
     own_sum(1, "b7")
     own_sum(0, "b7")
     q1_out(1)
-    q1_out(0)
-    ts(cf(20), ci(1), 4.0, NONE, A.is_equal, A.mult)
-    ts(cf(21), ci(1), 0.0, NONE, A.is_equal, A.mult)
-    ts(("W1", 0, 16), ("ON", 0, 16), cf(20), None, A.mult)
-    ts(("B2w", 0, 16), ("ON", 0, 16), cf(21), None, A.mult)
-    run(pieces("DS", [4, 8, 12], ("b7", 0, 64), 0, 8))
-    spread("DS", DSK, "W1", 16, 0, 4, "b4", "s", True)
-    spread("DS", DSK, "W1", 16, 4, 8, "b6", "v", True)
-    share("W1", "xW1", 16, NC, 16 + V)
-    own_sum(2, "b5")
-    own_sum(3, "b5")
-    number_to_place(("NF", 0, 128), 128, 16, 16 + V, NC)
-    ts(("EQ", 0, 128), ("EQ", 0, 128), -BIG, None, A.mult)
-    run(pieces("DS", [4, 8, 12], ("b5", 64, 128), 8, 16))
-    spread("DS", DSK, "W1", 16, 8, 12, "b7", "s", True)
-    spread("DS", DSK, "W1", 16, 12, 16, "b4", "v", True)
-    tt(("L2", 0, 128), ("mA", 0, 128), ("EQ", 0, 128), A.add)
+    for s in (2, 3):
+        pull(3, s, 1536, 2048, s == 3)
+    own_sum(2, "b7")
+    own_sum(3, "b7")
     q1_out(2)
+    for i, b in enumerate(("b4", "b5", "b6")):
+        points(4 * i, 4 * i + 4, b)
+    number_to_place(("NF", 0, 128), 128, 16, 16 + V, NC)
+    run(pieces("DS", SK, ("b7", 0, 128), 0, 16))
+    ts(("EQ", 0, 128), ("EQ", 0, 128), -BIG, None, A.mult)
+    tt(("L2", 0, 128), ("mA", 0, 128), ("EQ", 0, 128), A.add)
+    spread("DS", DSK, "W1", 16, 0, 4, "b4", "s", True)
+    spread("DS", DSK, "W1", 16, 4, 8, "b5", "v", True)
+    share("W1", "xW1", 16, NC, 16 + V)
+    spread("DS", DSK, "W1", 16, 8, 12, "b6", "s", True)
+    points(12, 16, "b7")
+    spread("DS", DSK, "W1", 16, 12, 16, "b7", "v", True)
+
+    bH, bL, bA = ("b4", "b1"), ("b6", "b6"), ("b5", "b5")
+    gather("s", "GA", GB[3], GB[3] + 2048, "W1", 0, OWN2, "L2")
+    gather("s", "GA", GB[3] + 2048, 8192, "W1", 0, OWN2, "L2")
+    gather("s", "GA", 0, GB[2], "W1", 0, HALO2, "L2")
+    fused_costs(K2, "L", 2, "W1", 0, OWN2, "L2", bL)
+    run(costs(K2, "H", 3, bH, (0, 1)))
+    first_half(K2, "H", bH)
+    run(costs(K2, "H", 3, bH, (2, 3)), best_of(K2, "L", bL))
+    spread("DB", BK, "B2w", 16, 4, 8, "b7", "s")
+    run(best_of(K2, "H", bH, True), costs(K2, "A", 0, bA))
+    spread("DB", BK, "B2w", 16, 8, 12, "b2", "s")
+    run(costs(K2, "A", 1, bA))
+    q1_out(0)
+    spread("DB", BK, "B2w", 16, 12, 16, "b7", "s")
     q1_out(3)
     for r in range(16):
         i, j = r // 4, r % 4
         k = 4 * min(i, j) + max(i, j)
         dma("y", T.q1[r::16, :], T.C1f[k::16, :], [("C1f", 0, V)], [("q1#%d" % r, 0, V)], "dq1", 16 * (r + 1))
-
-    gather("s", "GA", GB[3], GB[3] + 2048, "W1", 0, OWN2, "L2")
-    gather("s", "GA", 0, GB[2], "W1", 0, HALO2, "L2")
-    gather("s", "GA", GB[3] + 2048, 8192, "W1", 0, OWN2, "L2")
-    fused_costs(K2, "L", 2, "W1", 0, OWN2, "L2", "b6")
-    run(costs(K2, "H", 3, "b4", (0, 1)), best_of(K2, "L", "b6"))
-    spread("DB", BK, "B2w", 16, 4, 8, "b7", "s")
-    numbers(K2, "H", 3, "b4", (0, 1))
-    run(costs(K2, "A", 0, "b5"), costs(K2, "A", 1, "b5"))
-    run(costs(K2, "H", 3, "b4", (2, 3)), best_of(K2, "A", "b5"))
-    spread("DB", BK, "B2w", 16, 0, 4, "b3", "s")
+    run(best_of(K2, "A", bA))
+    spread("DB", BK, "B2w", 16, 0, 4, "b7", "v")
     share("B2w", "xB2", 16, NC, 16 + V)
-    run(best_of(K2, "H", "b4"), choice(K2, "L", "b6", "VK2"))
-    spread("DB", BK, "B2w", 16, 8, 12, "b7", "s")
-    spread("DB", BK, "B2w", 16, 12, 16, "b3", "v")
-    numbers(K2, "A", 0, "b5")
-    numbers(K2, "A", 1, "b5")
-    numbers(K2, "H", 3, "b4", (2, 3))
+    numbers(K2, "H", 3, bH)
+    numbers(K2, "A", 0, bA)
+    numbers(K2, "A", 1, bA)
     for b in range(16):
         l = ("TB", 128 * b, 128 * b + 128)
-        mm(("b2", 0, 128), ap(*l), T.Mw[:, b:V:16], b == 0, b == 15, [l, ("Mw", 0, V)])
+        mm(("b0", 0, 128), ap(*l), T.Mw[:, b:V:16], b == 0, b == 15, [l, ("Mw", 0, V)])
 
     gather("s", "GB", GB[3], GB[3] + 2048, "B2w", 0, OWN2, "L2")
     gather("s", "GB", GB[3] + 2048, 8192, "B2w", 0, OWN2, "L2")
-    gather("s", "GB", 0, GB[2], "B2w", 0, HALO2, "L2")
+    gather("s", "GB", 0, GB[1], "B2w", 0, HALO2, "L2")
     gather("s", "GB", GB[2], GB[3], "B2w", 0, OWN2, "L2")
-    run(choice(K2, "A", "b5", "VK2"), choice(K2, "H", "b4", "VK2"))
-    number_to_place(("b2", 0, 16), 16, 0, V, NB)
+    run(choice(K2, "H", bH, "VK2"), choice(K2, "L", bL, "VK2"))
+    number_to_place(("b0", 0, 16), 16, 0, V, NB)
     cp("v", ("LG", 0, 16), ("mA", 0, 16))
-    ts(("LG", 16, 128), ("b2", 16, 128), float(-own), None, A.add)
-    bests(K2, "H", 3, "b1")
-    run(move_of(K2, "H", "b1"))
-    spread("DM", MK, "M2w", 0, 8, 12, "b7", "v")
-    spread("DM", MK, "M2w", 0, 12, 16, "b3", "v")
+    ts(("LG", 16, 128), ("b0", 16, 128), float(-own), None, A.add)
+    bests(K2, "H", 3, "b2")
+    run(choice(K2, "A", bA, "VK2"))
+    run(move_of(K2, "H", "b2"))
+    gather("v", "GB", GB[1], GB[2], "B2w", 0, HALO2, "L2")
     bests(K2, "A", 0, "b0")
     bests(K2, "A", 1, "b0")
     run(move_of(K2, "A", "b0"))
     spread("DM", MK, "M2w", 0, 0, 4, "b5", "v")
     share("M2w", "xM2", 0, NB, V)
-    bests(K2, "L", 2, "b2")
-    run(move_of(K2, "L", "b2"))
-    spread("DM", MK, "M2w", 0, 4, 8, "b7", "v")
+    spread("DM", MK, "M2w", 0, 8, 12, "b7", "s")
+    spread("DM", MK, "M2w", 0, 12, 16, "b3", "s")
+    bests(K2, "L", 2, "b1")
+    run(move_of(K2, "L", "b1"))
+    spread("DM", MK, "M2w", 0, 4, 8, "b4", "v")
 
     gather("s", "GA", 1024, 2048, "M2w", 0, V, "LG")
     gather("v", "GA", 256, 1024, "M2w", 0, V, "LG")

from concourse.bass import DstId, RemoteDMATransfer
from concourse.mybir import AluOpType as A, ActivationFunctionType as F

N, V, NB, NC = 4, 2048, 256, 512
C0, CW, GB = [0, 256, 512, 1024], [256, 256, 512, 1024], [0, 1024, 2048, 4096]
HALO1, HALO2 = V + 3 * NB, 16 + V + 3 * NC
BIG = 65536.0
NONE = float(1 << 24)

SCRATCH = {}
for _n, _w, _t in (
        ("Qw", 16 + HALO1, "float32"), ("Pb", V, "bfloat16"), ("nbi", 512, "int32"), ("W", HALO1, "bfloat16"),
        ("W1", HALO2, "bfloat16"), ("Bw", HALO1, "bfloat16"), ("Mw", HALO1, "bfloat16"), ("B2w", HALO2, "bfloat16"),
        ("M2w", HALO1, "bfloat16"), ("L1", 512, "uint16"), ("LQ", 512, "uint16"), ("L2", 512, "uint16"), ("LG", 128, "uint16"),
        ("posq", 512, "float32"), ("VT", 512, "float32"), ("EQ", 512, "float32"), ("NF", 128, "float32"), ("mA", 128, "float32"),
        ("mB", 384, "float32"), ("GA", 8192, "bfloat16"), ("GB", 8192, "bfloat16"), ("GH", 8192, "float16"),
        ("PR", 8192, "float32"), ("PRS", V, "float32"), ("C1f", V, "float32"), ("DS", V, "bfloat16"), ("DB", V, "bfloat16"),
        ("DM", V, "bfloat16"), ("TB", V, "bfloat16"), ("ON", 512, "bfloat16"), ("Id", 128, "bfloat16"), ("PM", 128, "bfloat16"),
        ("PMh", 128, "float16"), ("PMf", 128, "float32"), ("PI", 128, "bfloat16"), ("E8", 8, "bfloat16"), ("wC", 8, "float32"),
        ("wS", 8, "float32"), ("wK", 32, "bfloat16"), ("wKf", 32, "float32"), ("ci", 8, "int32"), ("cf", 32, "float32"),
        ("VC", 128, "float32"), ("VK1", 512, "float32"), ("VK2", 512, "float32"), ("t1", 256, "float32"), ("t2", 256, "float32"),
        ("best", 128, "float32"), ("rem", 128, "float32"), ("E", 512, "float32"), ("X", 512, "float32"), ("X2", 256, "float32"),
        ("XI", 128, "int32"), ("CI", 128, "int32"), ("DD", 128, "float32"), ("Dh", 128, "bfloat16"), ("Dl", 128, "float32"),
        ("LT", 512, "float32"), ("tt", 512, "float32"), ("tm", 256, "float32"), ("tn", 128, "float32"), ("cl", 128, "float32"),
        ("GO", 128, "float32")):
    SCRATCH[_n] = ("sbuf", [128, _w], _t)
for _i in range(8):
    SCRATCH["b%d" % _i] = ("psum", [128, 512], "float32")
EX = ["xQ", "xW", "xB", "xM", "xW1", "xB2", "xM2"]
SEMAPHORES = ["v", "s", "p", "g", "rl", "dq1", "dgo"] + ["d%d" % i for i in range(9)] + EX


def make(g, T):
    QO = {"v": g.vector, "s": g.scalar, "p": g.tensor, "y": g.sync, "g": g}
    cnt = {"v": 0, "s": 0, "p": 0, "g": 0}
    known = {q: {} for q in QO}
    clk, acc = {}, {}

    def waits(q, toks):
        k = known[q]
        todo = {}
        for ch, n in toks:
            if k.get(ch, 0) < n:
                todo[ch] = max(n, todo.get(ch, 0))
        items = sorted(todo.items())
        for ch, n in items:
            if any(c2 != ch and clk[(c2, n2)].get(ch, 0) >= n for c2, n2 in items):
                continue
            QO[q].wait_ge(T.sem[ch], n)
            k[ch] = max(n, k.get(ch, 0))
            for c3, n3 in clk[(ch, n)].items():
                k[c3] = max(n3, k.get(c3, 0))

    def is_bank(key):
        return len(key) == 2 and key[0] == "b" and key[1].isdigit()

    def deps(q, r, w, isdma):
        toks = set()
        for lst, wr in ((r, False), (w, True)):
            for key, lo, hi in lst:
                bank = is_bank(key)
                for lo2, hi2, tok, q2, w2 in acc.get(key, []):
                    same = q2 == q and not isdma
                    if same and q == "p":
                        continue
                    if bank and not same:
                        toks.add(tok)
                        continue
                    if lo2 >= hi or lo >= hi2:
                        continue
                    if w2 or (wr and not same):
                        toks.add(tok)
        return toks

    def record(q, r, w, tok):
        for key, lo, hi in w:
            bank = is_bank(key)
            acc[key] = [a for a in acc.get(key, []) if not ((lo <= a[0] and a[1] <= hi) or (bank and a[3] != q))]
            acc[key].append((lo, hi, tok, q, True))
        for key, lo, hi in r:
            bank = is_bank(key)
            acc[key] = [a for a in acc.get(key, [])
                        if not ((not a[4] and a[3] == q and q in cnt and lo <= a[0] and a[1] <= hi) or (bank and a[3] != q))]
            acc[key].append((lo, hi, tok, q, False))

    def op(q, fn, r, w):
        waits(q, deps(q, r, w, False))
        cnt[q] += 1
        fn(QO[q]).then_inc(T.sem[q], 1)
        tok = (q, cnt[q])
        c = dict(known[q])
        c[q] = cnt[q]
        clk[tok] = c
        record(q, r, w, tok)

    def dma(q, out, in_, r, w, sem, total=16):
        waits(q, deps(q, r, w, True))
        QO[q].dma_start(out, in_).then_inc(T.sem[sem], 16)
        tok = (sem, total)
        c = dict(known[q])
        c[sem] = total
        clk[tok] = c
        record("d", r, w, tok)

    def arrives(sem, total, w):
        tok = (sem, total)
        clk[tok] = {sem: total}
        record("d", [], w, tok)

    def reads(q, r):
        waits(q, deps(q, r, [], True))

    def finish(q, toks):
        for ch in ("v", "s", "p", "g"):
            if cnt[ch]:
                toks.append((ch, cnt[ch]))
        for ch, n in toks:
            if known[q].get(ch, 0) < n or ch not in cnt:
                QO[q].wait_ge(T.sem[ch], n)
                known[q][ch] = n

    return op, dma, arrives, reads, finish


def run(*gens):
    gens = list(gens)
    while gens:
        left = []
        for x in gens:
            try:
                next(x)
                left.append(x)
            except StopIteration:
                pass
        gens = left


def rank_program(g, core, T, topo):
    rank = T.rank_of(core)
    if rank is None:
        return
    op, dma, arrives, reads, finish = make(g, T)
    own = V * rank
    others = [c for c in T.cores if c != core]
    R = range(4)

    def ap(b, lo, hi):
        return T[b][:, lo:hi]

    def tt(o, a, b, f):
        op("v", lambda e: e.tensor_tensor(ap(*o), ap(*a), ap(*b), f), [a, b], [o])

    def ts(o, a, s1, s2, f1, f2=None):
        rd = [a] + [x for x in (s1, s2) if isinstance(x, tuple)]
        x1 = ap(*s1) if isinstance(s1, tuple) else s1
        x2 = ap(*s2) if isinstance(s2, tuple) else s2
        if f2 is None:
            op("v", lambda e: e.tensor_scalar(ap(*o), ap(*a), x1, x2, f1), rd, [o])
        else:
            op("v", lambda e: e.tensor_scalar(ap(*o), ap(*a), x1, x2, f1, f2), rd, [o])

    def cp(q, o, a):
        if q == "v":
            op("v", lambda e: e.tensor_copy(ap(*o), ap(*a)), [a], [o])
        else:
            op("s", lambda e: e.activation(ap(*o), ap(*a), F.Copy), [a], [o])

    def scaled(o, a, col, bias=None):
        rd = [a, col] + ([bias] if bias else [])
        if bias:
            op("s", lambda e: e.activation(ap(*o), ap(*a), F.Identity, bias=ap(*bias), scale=ap(*col)), rd, [o])
        else:
            op("s", lambda e: e.activation(ap(*o), ap(*a), F.Identity, scale=ap(*col)), rd, [o])

    def dcol(d, k, b0, b1):
        return (d + "#%d" % k, 128 * b0, 128 * b1), T[d][:, 128 * b0 + k:128 * b1:16]

    def mm(o, lt, rh, start, stop, r):
        op("p", lambda e: e.matmul(ap(*o), lt, rh, start, stop), r, [o])

    def fill(b, lo, hi, x):
        op("v", lambda e: e.memset(ap(b, lo, hi), x), [], [(b, lo, hi)])

    for i in R:
        a = 512 * i
        dma("y", T.Qw[:, 16 + a:16 + a + 512], T.qu[:, a:a + 512], [], [("Qw", 16 + a, 16 + a + 512)], "d%d" % i)
        dma("s", T.Pb[:, a:a + 512], T.po[:, a:a + 512], [], [("Pb", a, a + 512)], "d%d" % (4 + i))
        if i == 0:
            dma("s", T.nbi[:], T.nb[:], [], [("nbi", 0, 512)], "d8")

    msk = topo.mask(core, others[0])
    for c in others[1:]:
        msk &= topo.mask(core, c)
    ne = bin(msk).count("1")
    sent = [0]
    arrives("xQ", 3 * ne, [("Qw", 16 + V, 16 + HALO1)])
    for b, x in (("W", "xW"), ("Bw", "xB"), ("Mw", "xM"), ("M2w", "xM2")):
        arrives(x, 3 * ne, [(b, V, HALO1)])
    for b, x in (("W1", "xW1"), ("B2w", "xB2")):
        arrives(x, 3 * ne, [(b, 16 + V, HALO2)])

    def share(b, sem, lo, w, base):
        reads("g", [(b, lo, lo + w)])
        ids, dst = [], []
        for c in others:
            q = T.rank_of(c)
            at = base + w * (rank if rank < q else rank - 1)
            rid, pid = topo.addr(c)[0], topo.addr(c)[1]
            ids.append(DstId(rid=rid, pnc=pid))
            dst.append(T[b][:, at:at + w])
        g.remote_dma_fused([RemoteDMATransfer(dst_ids=ids, dma_engine_mask=msk, remote_sem=T.sem[sem],
                                              srcs=[T[b][:, lo:lo + w]], dsts=dst)], local_sem=T.sem.rl)
        sent[0] += ne

    def g_sel(o, i, pat, c, base, cm):
        op("g", lambda e: e.affine_select(ap(*o), ap(*i), pat, c, 0.0, base, cm), [i], [o])

    def g_iota(o, pat, base, cm, fl=True, w=None):
        if fl:
            op("g", lambda e: e.iota(ap(*o), pat, base, cm, allow_small_or_imprecise_dtypes=True), [], w or [o])
        else:
            op("g", lambda e: e.iota(ap(*o), pat, base, cm), [], [o])

    def classes(d):
        return [(d + "#%d" % k, 0, V) for k in range(16)]

    def ci(k):
        return ("ci", k, k + 1)

    def cf(k):
        return ("cf", k, k + 1)

    fill("ON", 0, 512, 1.0)
    fill("Qw", 0, 16, 0.0)
    g_iota(ci(0), [[0, 1]], 0, 1, False)
    g_sel(("Id", 0, 128), ("ON", 0, 128), [[-1, 128]], A.is_equal, 0, 1)
    g_sel(("E8", 0, 8), ("ON", 0, 8), [[-16, 8]], A.is_ge, 0, 1)
    g_sel(("E8", 0, 8), ("E8", 0, 8), [[16, 8]], A.is_ge, 15, -1)
    g_iota(("VC", 0, 128), [[128, 16], [0, 8]], own, 1)
    for x in range(4):
        n = CW[x] // 16
        g_iota(("VT", GB[x] // 16, GB[x] // 16 + 4 * n), [[0, 4], [16, n]], own + C0[x], 0)
    share("Qw", "xQ", 16, NB, 16 + V)
    K1 = {"A": (0, 2, 0), "L": (2, 8, 64), "H": (8, 16, 256)}
    K2 = {"A": (0, 4, 0), "L": (4, 8, 128), "H": (8, 16, 256)}
    ts(ci(1), ci(0), 15, None, A.bitwise_and)
    op("v", lambda e: e.memset(T.DS[:], 0.0), [], classes("DS"))
    ts(ci(2), ci(1), 2, None, A.logical_shift_right)
    ts(ci(3), ci(1), 3, None, A.bitwise_and)
    cp("v", cf(0), ci(1))
    tt(cf(1), ci(3), ci(2), A.is_lt)
    tt(cf(3), ci(3), ci(2), A.is_gt)
    tt(cf(2), ci(3), ci(2), A.is_equal)
    ts(cf(4), cf(1), -1.0, 1.0, A.mult, A.add)
    ts(cf(5), ci(3), 0.0, cf(1), A.is_equal, A.mult)
    ts(cf(6), cf(3), 2.0, cf(2), A.mult, A.add)
    ts(cf(8), ci(1), 9.0, None, A.is_equal)
    tt(cf(7), cf(6), cf(5), A.add)
    ts(cf(9), ci(1), 13.0, cf(8), A.is_equal, A.add)
    for s in R:
        ts(cf(10 + s), ci(1), 14.0, 8192.0 * (3 - s), A.is_equal, A.mult)
    for s in R:
        tt(cf(10 + s), cf(10 + s), cf(9), A.add)
    ts(cf(20), ci(1), 4.0, NONE, A.is_equal, A.mult)
    ts(cf(21), ci(1), 0.0, NONE, A.is_equal, A.mult)
    scaled(("PM", 0, 128), ("Id", 0, 128), cf(4))
    scaled(("wS", 0, 8), ("E8", 0, 8), cf(6))
    scaled(("wC", 0, 8), ("E8", 0, 8), cf(7))
    for s in R:
        scaled(("wKf", 8 * s, 8 * s + 8), ("E8", 0, 8), cf(10 + s))
    cp("s", ("wK", 0, 32), ("wKf", 0, 32))
    scaled(("PMf", 0, 128), ("Id", 0, 128), cf(4))
    scaled(("PMh", 0, 128), ("Id", 0, 128), cf(4))
    scaled(("PI", 0, 128), ("Id", 0, 128), cf(1))
    scaled(("W1", 0, 16), ("ON", 0, 16), cf(20))
    scaled(("B2w", 0, 16), ("ON", 0, 16), cf(21))
    vt = ("VT", 0, 512)
    op("s", lambda e: e.activation(ap(*vt), ap(*vt), F.Identity, bias=ap(*cf(0))), [vt, cf(0)], [vt])
    vc = ("VC", 0, 128)
    k9, a9 = dcol("DS", 9, 0, 16)
    k13, a13 = dcol("DS", 13, 0, 16)
    k14, a14 = dcol("DS", 14, 0, 16)
    op("v", lambda e: e.tensor_copy(a9, ap(*vc)), [vc], [k9])
    op("v", lambda e: e.tensor_scalar(a14, ap(*vc), 0.0, 1.0, A.mult, A.add), [vc], [k14])
    op("v", lambda e: e.tensor_tensor(a13, ap(*vc), a9, A.subtract), [vc, k9], [k13])

    def number_to_place(src, n, base0, halo, h):
        off = [(base0 if k == rank else halo + h * (k if k < rank else k - 1)) - V * k for k in range(N)]
        st = [k for k in range(1, N) if off[k] != off[k - 1]]
        ts(("mA", 0, n), src, float(off[0]), None, A.add)
        for k in st:
            ts(("mB", 128 * (k - 1), 128 * (k - 1) + n), src, float(V * k), float(off[k] - off[k - 1]), A.is_ge, A.mult)
        for k in st:
            tt(("mA", 0, n), ("mA", 0, n), ("mB", 128 * (k - 1), 128 * (k - 1) + n), A.add)

    def own_place(x, s):
        t0, w, lo = 128 * s + C0[x] // 16, CW[x] // 16, GB[x] // 16
        a, o = ("EQ", t0, t0 + w), ("posq", lo + s * w, lo + (s + 1) * w)
        op("s", lambda e: e.activation(ap(*o), ap(*a), F.Identity, bias=float(16 - own)), [a], [o])

    def s_sum(bank, blks):
        for b in blks:
            src = ("PRS", 128 * b, 128 * b + 128)
            mm((bank, 8 * b, 8 * b + 8), ap(*src), T.wS[:], True, True, [src, ("wS", 0, 8)])

    def pieces(d, ks, src, b0, b1):
        rem = ("rem", 8 * b0, 8 * b1)
        for i, k in enumerate(ks):
            kk, aa = dcol(d, k, b0, b1)
            if i == len(ks) - 1:
                kp, pv = dcol(d, ks[i - 1], b0, b1)
                op("v", lambda e: e.tensor_tensor(aa, ap(*src), pv, A.subtract), [src, kp], [kk])
            else:
                op("v", lambda e: e.tensor_copy(aa, ap(*src)), [src], [kk])
                yield
                if i < len(ks) - 2:
                    op("v", lambda e: e.tensor_tensor(ap(*rem), ap(*src), aa, A.subtract), [src, kk], [rem])
                    src = rem
            yield

    def points(b0, b1, bank):
        src = ("Pb", 128 * b0, 128 * b1)
        mm((bank, 0, 128 * (b1 - b0)), T.PM[:], ap(*src), True, False, [src, ("PM", 0, 128)])

    def spread(d, ks, win, base, b0, b1, bank, q, with_p=False):
        o = (bank, 0, 128 * (b1 - b0))
        for b in range(b0, b1):
            mm((bank, 128 * (b - b0), 128 * (b - b0) + 128), T[d][:, 128 * b:128 * b + 128], T.Id[:], not with_p,
               (b == b1 - 1) or not with_p, [(d + "#%d" % k, 128 * b, 128 * b + 128) for k in ks] + [("Id", 0, 128)])
        cp(q, (win, base + 128 * b0, base + 128 * b1), o)

    DSK, SK = [4, 8, 12, 9, 13, 14], [4, 8, 12]
    for i in R:
        q = ("Qw", 16 + 512 * i, 528 + 512 * i)
        c = ("C1f", 512, 1024) if i == 1 else ("b%d" % i, 0, 512)
        scaled(c, q, cf(4), cf(1))
        tt(("PRS", 512 * i, 512 * i + 512), ("Pb", 512 * i, 512 * i + 512), c, A.mult)
        s_sum(("b4", "b4", "b5", "b5")[i], range(4 * i, 4 * i + 4))
        if i == 0:
            cp("v", ("EQ", 0, 512), ("nbi", 0, 512))
        if i == 1:
            for x in (1, 2, 3):
                for s in R:
                    own_place(x, s)
            for s in R:
                cp("s", ("NF", 16 * s, 16 * s + 16), ("EQ", 128 * s, 128 * s + 16))
            points(0, 4, "b6")
            points(4, 8, "b7")
            run(pieces("DS", SK, ("b4", 0, 64), 0, 8))
            spread("DS", DSK, "W", 0, 0, 4, "b6", "s", True)
            spread("DS", DSK, "W", 0, 4, 8, "b7", "v", True)
            share("W", "xW", 0, NB, V)
    points(8, 12, "b4")
    points(12, 16, "b6")
    number_to_place(("NF", 0, 64), 64, 0, V, NB)
    run(pieces("DS", SK, ("b5", 64, 128), 8, 16))
    ts(("L1", 128, 512), ("posq", 128, 512), float(-16 - NB), None, A.add)
    ts(("L1", 64, 128), ("posq", 64, 128), -16.0, None, A.add)
    cp("v", ("L1", 0, 64), ("mA", 0, 64))
    spread("DS", DSK, "W", 0, 8, 12, "b4", "s", True)
    spread("DS", DSK, "W", 0, 12, 16, "b6", "v", True)
    ts(("posq", 0, 64), ("mA", 0, 64), 16.0, None, A.add)

    g_iota(("DB", 0, V), [[0, V]], 0, 0, True, classes("DB"))
    for nm, K in (("VK1", K1), ("VK2", K2)):
        for ch in "HLA":
            b0, b1, o = K[ch]
            g_iota((nm, o, o + 32 * (b1 - b0)), [[-8192, 4], [128, b1 - b0], [0, 8]], own + 3 * 8192 + 128 * b0, 1)
        if nm == "VK1":
            g_iota(("TB", 0, V), [[0, V]], 0, 0)
            g_iota(("DM", 0, V), [[0, V]], 0, 0, True, classes("DM"))

    def gather(q, out, lo, hi, win, w0, w1, offs):
        o, wn, of = (out, lo, hi), (win, w0, w1), (offs, lo // 16, hi // 16)
        if q == "v":
            op("v", lambda e: e.tensor_copy(ap(*o), ap(*wn).indirect(ap(*of))), [wn, of], [o])
        else:
            op("s", lambda e: e.activation(ap(*o), ap(*wn).indirect(ap(*of)), F.Copy), [wn, of], [o])

    def fused(lo, hi, win, w0, w1, offs, c0, c1):
        o, wn, of, c = ("PR", lo, hi), (win, w0, w1), (offs, lo // 16, hi // 16), ("C1f", c0, c1)
        op("v", lambda e: e.tensor_tensor(ap(*o), ap(*wn).indirect(ap(*of)), ap(*c), A.mult), [wn, of, c], [o])

    def sums(src, w, x, s, c0, c1, bank, col, n, b0):
        for b in range(c0 // 128, c1 // 128):
            lo = GB[x] + s * CW[x] + 128 * b - C0[x]
            at = col + s * n + 8 * (b - b0)
            sr = (src, lo, lo + 128)
            mm((bank, at, at + 8), ap(*sr), ap(*w), True, True, [sr, w])

    def costs(K, ch, x, banks, slots=R):
        b0, b1, _ = K[ch]
        for s in slots:
            for c0 in range(C0[x], C0[x] + CW[x], 512):
                k, w = c0 // 512, min(512, CW[x])
                lo = GB[x] + s * CW[x] + c0 - C0[x]
                tt(("PR", lo, lo + w), ("GA", lo, lo + w), ("b%d" % k, c0 - 512 * k, c0 - 512 * k + w), A.mult)
                sums("PR", wC, x, s, c0, c0 + w, banks[s // 2], 0, 8 * (b1 - b0), b0)
                yield

    def fused_costs(K, ch, x, win, w0, w1, offs, banks):
        b0, b1, _ = K[ch]
        for s in R:
            lo = GB[x] + s * CW[x]
            fused(lo, lo + CW[x], win, w0, w1, offs, C0[x], C0[x] + CW[x])
            sums("PR", wC, x, s, C0[x], C0[x] + CW[x], banks[s // 2], 0, 8 * (b1 - b0), b0)
            sums("PR", ("wKf", 8 * s, 8 * s + 8), x, s, C0[x], C0[x] + CW[x], banks[0], 256, 8 * (b1 - b0), b0)

    def numbers(K, ch, x, banks):
        b0, b1, _ = K[ch]
        for s in R:
            sums("GA", ("wK", 8 * s, 8 * s + 8), x, s, C0[x], C0[x] + CW[x], banks[0], 256, 8 * (b1 - b0), b0)

    def bests(K, ch, x, bank):
        b0, b1, _ = K[ch]
        for s in R:
            sums("GB", E8, x, s, C0[x], C0[x] + CW[x], bank, 0, 8 * (b1 - b0), b0)

    def first_half(K, ch, banks):
        b0, b1, o = K[ch]
        n, h = 8 * (b1 - b0), o // 2
        cp("v", ("t1", h, h + 2 * n), (banks[0], 0, 2 * n))

    def best_of(K, ch, banks, half_done=False):
        b0, b1, o = K[ch]
        n, h = 8 * (b1 - b0), o // 2
        be = ("best", 8 * b0, 8 * b1)
        if not half_done:
            first_half(K, ch, banks)
            yield
        tt(("t2", h, h + 2 * n), (banks[1], 2 * n, 4 * n), ("t1", h, h + 2 * n), A.min)
        yield
        tt(be, ("t2", h, h + n), ("t2", h + n, h + 2 * n), A.min)
        yield
        yield from pieces("DB", BK, be, b0, b1)

    def choice(K, ch, banks, vk):
        b0, b1, o = K[ch]
        n, h = 8 * (b1 - b0), o // 2
        c = (8 * b0, 8 * b1)
        be = ("best",) + c
        kk = (banks[0], 256, 256 + 4 * n)
        for s in R:
            tt(("E", o + s * n, o + (s + 1) * n), (banks[s // 2], s * n, (s + 1) * n), be, A.is_equal)
            yield
        tt(("LT", o, o + 4 * n), kk, (vk, o, o + 4 * n), A.is_gt)
        yield
        tt(("X", o, o + 4 * n), kk, ("E", o, o + 4 * n), A.mult)
        yield
        tt(("X2", h, h + 2 * n), ("X", o, o + 2 * n), ("X", o + 2 * n, o + 4 * n), A.max)
        yield
        tt(("XI",) + c, ("X2", h, h + n), ("X2", h + n, h + 2 * n), A.max)
        yield
        ts(("CI",) + c, ("XI",) + c, 8191, None, A.bitwise_and)
        yield
        tt(("DD",) + c, ("CI",) + c, ("VC",) + c, A.subtract)
        yield
        cp("v", ("Dh",) + c, ("DD",) + c)
        yield
        tt(("Dl",) + c, ("DD",) + c, ("Dh",) + c, A.subtract)
        yield

    def move_of(K, ch, bank):
        b0, b1, o = K[ch]
        n, h = 8 * (b1 - b0), o // 2
        c = (8 * b0, 8 * b1)
        tt(("tt", o, o + 4 * n), (bank, 0, 4 * n), ("LT", o, o + 4 * n), A.add)
        yield
        tt(("tm", h, h + 2 * n), ("tt", o, o + 2 * n), ("tt", o + 2 * n, o + 4 * n), A.min)
        yield
        tt(("tn",) + c, ("tm", h, h + n), ("tm", h + n, h + 2 * n), A.min)
        yield
        tt(("cl",) + c, ("tn",) + c, ("best",) + c, A.is_gt)
        yield
        for k, d in ((0, "Dh"), (1, "Dl")):
            kk, aa = dcol("DM", k, b0, b1)
            op("v", lambda e: e.tensor_tensor(aa, ap(*(("cl",) + c)), ap(*((d,) + c)), A.mult), [("cl",) + c, (d,) + c], [kk])
            yield

    def start_q1(i):
        o, a = ("b%d" % i, 0, 512), ("Qw", 16 + 512 * i, 528 + 512 * i)
        mm(o, T.PMf[:], ap(*a), True, False, [a, ("PMf", 0, 128)])
        mm(o, T.PI[:], T.ON[:], False, False, [("PI", 0, 128), ("ON", 0, 512)])

    def weights_of_tables():
        for b in range(16):
            o, a = T.TB[:, 129 * b:128 * b + 128:16], T.E8[:]
            op("s", lambda e: e.activation(o, a, F.Copy), [E8], [("TB", 128 * b, 128 * b + 128)])

    wC, E8 = ("wC", 0, 8), ("E8", 0, 8)
    BK, MK = [0, 1, 2], [0, 1, 2, 3]

    bH, bL, bA = ("b4", "b1"), ("b5", "b5"), ("b3", "b3")
    gather("s", "GA", GB[3], GB[3] + 2048, "W", NB, V, "L1")
    gather("s", "GA", GB[1], GB[2], "W", 0, V, "L1")
    gather("s", "GA", GB[3] + 2048, 8192, "W", NB, V, "L1")
    gather("s", "GA", 0, GB[1], "W", 0, HALO1, "L1")
    weights_of_tables()
    fused_costs(K1, "L", 2, "W", NB, V, "L1", bL)
    run(costs(K1, "H", 3, bH, (0, 1)))
    run(costs(K1, "L", 1, bL))
    first_half(K1, "H", bH)
    run(costs(K1, "H", 3, bH, (2, 3)), best_of(K1, "L", bL))
    spread("DB", BK, "Bw", 0, 4, 8, "b6", "s")
    spread("DB", BK, "Bw", 0, 2, 4, "b7", "s")
    numbers(K1, "L", 1, bL)
    run(best_of(K1, "H", bH, True))
    spread("DB", BK, "Bw", 0, 8, 12, "b6", "s")
    spread("DB", BK, "Bw", 0, 12, 16, "b7", "v")
    run(costs(K1, "A", 0, bA))

    gather("s", "GB", GB[3], GB[3] + 2048, "Bw", NB, V, "L1")
    gather("s", "GB", GB[3] + 2048, 8192, "Bw", NB, V, "L1")
    gather("s", "GB", GB[2], GB[3], "Bw", NB, V, "L1")
    run(best_of(K1, "A", bA))
    numbers(K1, "H", 3, bH)
    numbers(K1, "A", 0, bA)
    spread("DB", BK, "Bw", 0, 0, 2, "b6", "v")
    share("Bw", "xB", 0, NB, V)
    for k, j in ((2, 9), (3, 13)):
        kk, aa = dcol("DM", k, 0, 16)
        ks, sv = dcol("DS", j, 0, 16)
        op("v", lambda e: e.tensor_copy(aa, sv), [ks], [kk])
    gather("s", "GB", GB[1], GB[2], "Bw", 0, V, "L1")
    run(choice(K1, "H", bH, "VK1"), choice(K1, "L", bL, "VK1"))
    bests(K1, "H", 3, "b2")
    bests(K1, "L", 2, "b0")
    run(move_of(K1, "H", "b2"), choice(K1, "A", bA, "VK1"))
    spread("DM", MK, "Mw", 0, 8, 12, "b6", "v")
    spread("DM", MK, "Mw", 0, 12, 16, "b7", "v")
    start_q1(2)
    bests(K1, "L", 1, "b0")
    gather("s", "GB", 0, GB[1], "Bw", 0, HALO1, "L1")
    bests(K1, "A", 0, "b1")
    run(move_of(K1, "L", "b0"))
    spread("DM", MK, "Mw", 0, 4, 8, "b6", "s")
    spread("DM", MK, "Mw", 0, 2, 4, "b7", "v")
    run(move_of(K1, "A", "b1"))
    spread("DM", MK, "Mw", 0, 0, 2, "b6", "v")
    for i in (3, 0, 1):
        start_q1(i)
    share("Mw", "xM", 0, NB, V)

    def tables(lo, hi, bank):
        o = (bank, lo // 16, hi // 16)
        for b in range(16):
            l = ("TB", 128 * b, 128 * b + 128)
            mm(o, ap(*l), T.GA[:, lo + b:hi:16], b == 0, b == 15, [l, ("GA", lo, hi)])

    def pull_list(lo, hi, bank):
        tt(("EQ", lo, hi), (bank, lo, hi), ("VT", lo, hi), A.is_equal)
        yield
        tt(("LQ", lo, hi), ("EQ", lo, hi), ("posq", lo, hi), A.mult)
        yield

    def next_list(lo, hi, bank):
        ts(("EQ", lo, hi), ("EQ", lo, hi), -BIG, float(16 - own), A.mult, A.add)
        yield
        tt(("L2", lo, hi), (bank, lo, hi), ("EQ", lo, hi), A.add)
        yield

    def pull(x, s, c0, c1, stop):
        k, lo = c0 // 512, GB[x] + s * CW[x] + c0 - C0[x]
        a = ("GH", lo, lo + c1 - c0)
        mm(("b%d" % k, c0 - 512 * k, c1 - 512 * k), T.PMh[:], ap(*a), False, stop, [a, ("PMh", 0, 128)])

    def q1_out(i):
        cp("s", ("C1f", 512 * i, 512 * i + 512), ("b%d" % i, 0, 512))

    def own_sum(i, bank):
        tt(("PRS", 512 * i, 512 * i + 512), ("Pb", 512 * i, 512 * i + 512), ("b%d" % i, 0, 512), A.mult)
        s_sum(bank, range(4 * i, 4 * i + 4))

    OWN2 = 16 + V
    gather("s", "GA", GB[3], GB[3] + 2048, "Mw", NB, V, "L1")
    gather("s", "GA", GB[3] + 2048, 8192, "Mw", NB, V, "L1")
    gather("s", "GA", 0, GB[1], "Mw", 0, HALO1, "L1")
    gather("v", "GA", GB[2], GB[3], "Mw", NB, V, "L1")
    gather("v", "GA", GB[1], GB[2], "Mw", 0, V, "L1")
    tables(GB[2], GB[3], "b5")
    tables(GB[3], GB[3] + 2048, "b4")
    tables(GB[1], GB[2], "b7")
    tables(GB[3] + 2048, 8192, "b6")
    run(pull_list(128, 256, "b5"))
    run(pull_list(256, 384, "b4"))
    run(pull_list(64, 128, "b7"))
    gather("s", "GH", GB[2], GB[3], "Qw", 0, OWN2, "LQ")
    gather("v", "GH", GB[3], GB[3] + 2048, "Qw", 0, OWN2, "LQ")
    tables(0, GB[1], "b7")
    run(pull_list(384, 512, "b6"), pull_list(0, 64, "b7"))
    gather("s", "GH", GB[1], GB[2], "Qw", 0, OWN2, "LQ")
    gather("v", "GH", 0, GB[1], "Qw", 0, 16 + HALO1, "LQ")
    run(next_list(384, 512, "b6"), next_list(128, 256, "b5"))
    run(next_list(256, 384, "b4"))
    cp("v", ("NF", 0, 128), ("b7", 0, 128))
    for c in (0, 512):
        for s in (2, 3):
            lo = GB[3] + 1024 * s + c
            gather("s", "GH", lo, lo + 512, "Qw", 0, OWN2, "LQ")
    for s in R:
        pull(2, s, 512, 1024, s == 3)
    for s in (0, 1):
        for c in (1024, 1536):
            pull(3, s, c, c + 512, False)
    for s in R:
        pull(1, s, 256, 512, False)
    for s in R:
        pull(0, s, 0, 256, s == 3)

    for s in (2, 3):
        pull(3, s, 1024, 1536, s == 3)
    own_sum(1, "b7")
    own_sum(0, "b7")
    q1_out(1)
    for s in (2, 3):
        pull(3, s, 1536, 2048, s == 3)
    own_sum(2, "b7")
    own_sum(3, "b7")
    q1_out(2)
    for i, b in enumerate(("b4", "b5", "b6")):
        points(4 * i, 4 * i + 4, b)
    number_to_place(("NF", 0, 128), 128, 16, 16 + V, NC)
    run(pieces("DS", SK, ("b7", 0, 128), 0, 16))
    ts(("EQ", 0, 128), ("EQ", 0, 128), -BIG, None, A.mult)
    tt(("L2", 0, 128), ("mA", 0, 128), ("EQ", 0, 128), A.add)
    spread("DS", DSK, "W1", 16, 0, 4, "b4", "s", True)
    spread("DS", DSK, "W1", 16, 4, 8, "b5", "v", True)
    share("W1", "xW1", 16, NC, 16 + V)
    spread("DS", DSK, "W1", 16, 8, 12, "b6", "s", True)
    points(12, 16, "b7")
    spread("DS", DSK, "W1", 16, 12, 16, "b7", "v", True)

    bH, bL, bA = ("b4", "b1"), ("b6", "b6"), ("b5", "b5")
    gather("s", "GA", GB[3], GB[3] + 2048, "W1", 0, OWN2, "L2")
    gather("s", "GA", GB[3] + 2048, 8192, "W1", 0, OWN2, "L2")
    gather("s", "GA", 0, GB[2], "W1", 0, HALO2, "L2")
    fused_costs(K2, "L", 2, "W1", 0, OWN2, "L2", bL)
    run(costs(K2, "H", 3, bH, (0, 1)))
    first_half(K2, "H", bH)
    run(costs(K2, "H", 3, bH, (2, 3)), best_of(K2, "L", bL))
    spread("DB", BK, "B2w", 16, 4, 8, "b7", "s")
    run(best_of(K2, "H", bH, True), costs(K2, "A", 0, bA))
    spread("DB", BK, "B2w", 16, 8, 12, "b2", "s")
    run(costs(K2, "A", 1, bA))
    q1_out(0)
    spread("DB", BK, "B2w", 16, 12, 16, "b7", "s")
    q1_out(3)
    for r in range(16):
        i, j = r // 4, r % 4
        k = 4 * min(i, j) + max(i, j)
        dma("y", T.q1[r::16, :], T.C1f[k::16, :], [("C1f", 0, V)], [("q1#%d" % r, 0, V)], "dq1", 16 * (r + 1))
    run(best_of(K2, "A", bA))
    spread("DB", BK, "B2w", 16, 0, 4, "b7", "v")
    share("B2w", "xB2", 16, NC, 16 + V)
    numbers(K2, "H", 3, bH)
    numbers(K2, "A", 0, bA)
    numbers(K2, "A", 1, bA)
    for b in range(16):
        l = ("TB", 128 * b, 128 * b + 128)
        mm(("b0", 0, 128), ap(*l), T.Mw[:, b:V:16], b == 0, b == 15, [l, ("Mw", 0, V)])

    gather("s", "GB", GB[3], GB[3] + 2048, "B2w", 0, OWN2, "L2")
    gather("s", "GB", GB[3] + 2048, 8192, "B2w", 0, OWN2, "L2")
    gather("s", "GB", 0, GB[1], "B2w", 0, HALO2, "L2")
    gather("s", "GB", GB[2], GB[3], "B2w", 0, OWN2, "L2")
    run(choice(K2, "H", bH, "VK2"), choice(K2, "L", bL, "VK2"))
    number_to_place(("b0", 0, 16), 16, 0, V, NB)
    cp("v", ("LG", 0, 16), ("mA", 0, 16))
    ts(("LG", 16, 128), ("b0", 16, 128), float(-own), None, A.add)
    bests(K2, "H", 3, "b2")
    run(choice(K2, "A", bA, "VK2"))
    run(move_of(K2, "H", "b2"))
    gather("v", "GB", GB[1], GB[2], "B2w", 0, HALO2, "L2")
    bests(K2, "A", 0, "b0")
    bests(K2, "A", 1, "b0")
    run(move_of(K2, "A", "b0"))
    spread("DM", MK, "M2w", 0, 0, 4, "b5", "v")
    share("M2w", "xM2", 0, NB, V)
    spread("DM", MK, "M2w", 0, 8, 12, "b7", "s")
    spread("DM", MK, "M2w", 0, 12, 16, "b3", "s")
    bests(K2, "L", 2, "b1")
    run(move_of(K2, "L", "b1"))
    spread("DM", MK, "M2w", 0, 4, 8, "b4", "v")

    gather("s", "GA", 1024, 2048, "M2w", 0, V, "LG")
    gather("v", "GA", 256, 1024, "M2w", 0, V, "LG")
    gather("v", "GA", 0, 256, "M2w", 0, HALO1, "LG")
    order = [8, 9, 10, 11, 12, 13, 14, 15, 2, 3, 4, 5, 6, 7, 0, 1]
    for b in order:
        l, a = ("TB", 128 * b, 128 * b + 128), ("GA", 128 * b, 128 * b + 128)
        mm(("b6", 0, 128), ap(*l), ap(*a), b == order[0], b == order[-1], [l, a])
    cp("v", ("GO", 0, 128), ("b6", 0, 128))
    dma("y", T.goal[:], T.GO[:], [("GO", 0, 128)], [("goal", 0, V)], "dgo")

    finish("y", [("dq1", 256), ("dgo", 16)])
    finish("g", [("rl", sent[0])] + [("d%d" % i, 16) for i in range(9)] + [(x, 3 * ne) for x in EX])
